import numpy as np
import ml_dtypes


def mxq(x, axis, fmt="e4m3"):
    dtype, down = {"e4m3": (ml_dtypes.float8_e4m3fn, 7), "e5m2": (ml_dtypes.float8_e5m2, 14)}[fmt]
    v = np.moveaxis(np.asarray(x, np.float32).astype(ml_dtypes.bfloat16).astype(np.float64), axis, -1)
    blocks = v.reshape(v.shape[:-1] + (-1, 32))
    amax = np.abs(blocks).max(-1, keepdims=True)
    byte = np.maximum(np.where(amax > 0, np.frexp(amax)[1] - 1 + 127, 0) - down, 1)
    scale = np.exp2(byte - 127.0)
    codes = (blocks / scale).astype(np.float32).astype(dtype).astype(np.float64)
    return np.moveaxis((codes * scale).reshape(v.shape), -1, axis)


WIDE = False


def mx_kscale(k):
    if not WIDE:
        return np.ones(k)
    levels = np.array([10, -10, 5, -5, 0])
    if k % 512:
        return np.exp2(np.random.permutation(np.resize(levels, k // 32))).repeat(32)
    a = np.empty((k // 512, 16))
    for p in range(k // 512):
        a[p, :8] = np.random.permutation(np.resize(levels, 8))
        for g in range(8):
            far = levels[np.abs(levels - a[p, g]) >= 10]
            a[p, g + 8] = far[np.random.randint(len(far))]
    return np.exp2(a.ravel()).repeat(32)


def f64(x):
    return np.asarray(x).astype(np.float64)


def striped(idx):
    return np.tile(idx.reshape(-1, 16).T, (8, 1)).astype(np.uint16)


def unstriped(offs):
    return offs[:16].T.reshape(-1).astype(np.int64)


E2M1 = np.array([0.0, 0.5, 1.0, 1.5, 2.0, 3.0, 4.0, 6.0, -0.0, -0.5, -1.0, -1.5, -2.0, -3.0, -4.0, -6.0])


def pack_weight(w, fmt):
    k, n = w.shape
    w = f64(np.asarray(w, np.float32).astype(ml_dtypes.bfloat16)).reshape(k // 32, 32, n)
    amax = np.abs(w).max(1)
    if fmt == "e4m3":
        byte = np.frexp(amax)[1] - 1 + 127 - 7
    else:
        mant, ex = np.frexp(amax / 6.0)
        byte = np.where(mant > 0.5, ex, ex - 1) + 127
    byte = np.clip(np.where(amax > 0, byte, 1), 1, 254)
    scaled = (w * np.exp2(127.0 - byte)[:, None, :]).reshape(k, n).astype(np.float32)
    by_word = np.ascontiguousarray(scaled.reshape(k // 512, 128, 4, n).transpose(0, 1, 3, 2))
    if fmt == "e4m3":
        words = by_word.astype(ml_dtypes.float8_e4m3fn).view(np.uint8)
    else:
        c = by_word.astype(ml_dtypes.float4_e2m1fn).view(np.uint8) & 0xF
        words = (c[..., 0::2] | (c[..., 1::2] << 4)).reshape(k // 512, 128, 2 * n)
    return np.ascontiguousarray(words), np.ascontiguousarray(byte.astype(np.uint8).reshape(k // 512, 16, n))


def unpack_weight(words, scales, fmt):
    g, _, n = scales.shape
    words = np.ascontiguousarray(words).reshape(g, 128, n, -1)
    if fmt == "e4m3":
        vals = words.view(ml_dtypes.float8_e4m3fn).astype(np.float64)
    else:
        nib = np.empty((g, 128, n, 4), np.uint8)
        nib[..., 0::2] = words & 0xF
        nib[..., 1::2] = words >> 4
        vals = E2M1[nib]
    vals = vals * np.repeat(np.exp2(scales.astype(np.float64) - 127.0), 8, axis=1)[..., None]
    return vals.transpose(0, 1, 3, 2).reshape(g * 512, n)


def pack_table(v):
    words, scales = pack_weight(v, "e4m3")
    return np.concatenate([words.reshape(words.shape[0], -1), scales.reshape(scales.shape[0], -1)], axis=1)


def unpack_table(tab):
    g, t = tab.shape[0], tab.shape[1] // 528
    return unpack_weight(tab[:, :512 * t].reshape(g, 128, t, 4), tab[:, 512 * t:].reshape(g, 16, t), "e4m3")


def silu(v):
    return v / (1.0 + np.exp(-np.maximum(v, -700.0)))


K, L, M, T, S = 1024, 1536, 128, 2048, 1024


def setup_inputs():
    n = np.random.standard_normal
    s1 = mx_kscale(K)[:, None]
    s2 = mx_kscale(L)[:, None]
    p_w4 = pack_weight(n((K, M)) / np.sqrt(K) / s1, "e2m1")
    return {
        "tab": pack_table(n((K, T)) * s1),
        "w4_words": p_w4[0],
        "w4_scales": p_w4[1],
        "x": (n((L, S)) * s2).astype(np.float32),
        "u": (n((L, M)) / np.sqrt(L) / s2).astype(np.float32),
        "b": (0.3 * n(128)).astype(np.float32),
        "offs": striped(np.random.permutation(T)[:S]),
    }


def reference(tab, w4_words, w4_scales, x, u, b, offs):
    tab_ = unpack_table(tab)[:, unstriped(offs)]
    w4_ = unpack_weight(w4_words, w4_scales, "e2m1")
    x_ = mxq(f64(x), 0, "e4m3")
    u_ = mxq(f64(u), 0, "e4m3")
    y = tab_.T @ w4_ + x_.T @ u_
    return silu(y + f64(b)[None, :])

@@ -1,0 +1,212 @@
+from contextlib import ExitStack
+
+import concourse.mybir as mybir
+from concourse.masks import make_identity
+
+K, L, M, T, S = 1024, 1536, 128, 2048, 1024
+FLOPS = 2 * S * M * (K + L)
+
+F32 = mybir.dt.float32
+BF16 = mybir.dt.bfloat16
+I32 = mybir.dt.int32
+U32 = mybir.dt.uint32
+U16 = mybir.dt.uint16
+U8 = mybir.dt.uint8
+FP8X4 = mybir.dt.float8_e4m3fn_x4
+FP4X4 = mybir.dt.float4_e2m1fn_x4
+SILU = mybir.ActivationFunctionType.Silu
+ADD = mybir.AluOpType.add
+
+P = 128
+KP = 512
+A = K // KP
+G = L // KP
+NT = S // P
+
+
+def tile_list_tabx_tm_silu_kernel(tc, tab, w4_words, w4_scales, x, u, b, offs, out):
+    nc = tc.nc
+
+    with ExitStack() as ctx:
+        keep = ctx.enter_context(tc.tile_pool(name="keep", bufs=1))
+        psum = ctx.enter_context(tc.psum_pool(name="psum", bufs=1))
+
+        offsets = keep.tile([P, S // 16], U16, name="offsets")
+        u_raw = keep.tile([P, G, 4, M], F32, name="u_raw", align_bytes=64)
+        tab_sc = keep.tile([P, A, T // 4], I32, name="tab_sc", align_bytes=64)
+        words = [keep.tile([P, T], I32, name=f"words{a}", align_bytes=64) for a in range(A)]
+        w4_w = keep.tile([P, A, 2 * M], U8, name="w4_w", align_bytes=64)
+        w4_s = keep.tile([P, A, M // 4], I32, name="w4_s", align_bytes=64)
+        b_row = keep.tile([P, M], F32, name="b_row", align_bytes=64)
+        b_col = keep.tile([P, 1], F32, name="b_col", align_bytes=64)
+        ident = keep.tile([P, P], F32, name="ident", align_bytes=64)
+        warm = keep.tile([P, 1], F32, name="warm", align_bytes=64)
+        warm2 = keep.tile([P, 1], F32, name="warm2", align_bytes=64)
+
+        tab_i = tab.bitcast(I32)
+        nc.vector.memset(tab_sc[:], 0)
+        nc.vector.memset(w4_s[:], 0)
+        nc.gpsimd.memset(warm[:], 0.0)
+        nc.gpsimd.memset(b_row[:], 0.0)
+
+        def load_words(a):
+            nc.sync.dma_start(out=words[a][:], in_=tab_i[a, 0 : 128 * T].rearrange("(p t) -> p t", p=P))
+
+        def load_scales(tile, rows):
+            view = rows.rearrange("a (q r) n -> r q a n", r=4)
+            for r in range(4):
+                nc.sync.dma_start(out=tile[r:P:32], in_=view[r])
+
+        x_raw = {}
+
+        def load_x(g, w0, w1):
+            t = keep.tile([P, 4, w1 - w0], F32, name=f"x_raw{g}_{w0}", align_bytes=64)
+            nc.sync.dma_start(out=t[:], in_=x[KP * g : KP * (g + 1), w0:w1].rearrange("(p j) w -> p j w", j=4))
+            x_raw[g, w0] = t
+
+        load_words(0)
+        nc.sync.dma_start(offsets[:], offs)
+        nc.sync.dma_start(out=b_row[0:1, :], in_=b.rearrange("(o n) -> o n", o=1))
+        load_scales(tab_sc, tab_i[:, 128 * T : 132 * T].rearrange("a (q t) -> a q t", q=16))
+        nc.sync.dma_start(out=u_raw[:], in_=u.rearrange("(g p j) n -> p g j n", p=P, j=4))
+        load_x(0, 0, S)
+        nc.sync.dma_start(out=w4_w[:].bitcast(I32), in_=w4_words.bitcast(I32).rearrange("a p n -> p a n"))
+        load_scales(w4_s, w4_scales.bitcast(I32))
+        load_words(1)
+        load_x(1, 0, S)
+        load_x(2, 0, 768)
+        load_x(2, 768, 1024)
+
+        make_identity(nc, ident[:])
+        nc.scalar.activation(warm2[:], warm[:], SILU)
+
+        def interleave(dst, src, w0, w1, by):
+            if w1 > w0:
+                o = dst[:, w0:w1, :].rearrange("p (c i) j -> p c j i", i=4)
+                s = src[:, :, w0:w1].rearrange("p j (c i) -> p c j i", i=4)
+                if by == "S":
+                    nc.scalar.copy(o, s)
+                else:
+                    nc.vector.tensor_copy(o, s)
+
+        u_bf = keep.tile([P, G, M, 4], BF16, name="u_bf", align_bytes=64)
+        u_c = keep.tile([P, G, M], U32, name="u_c", align_bytes=64)
+        u_s = keep.tile([P, G, M], U8, name="u_s", align_bytes=64)
+        for g in range(G):
+            interleave(u_bf[:, g], u_raw[:, g], 0, M, "S")
+        for g in range(G):
+            nc.vector.quantize_mx(
+                out=u_c[:, g].bitcast(FP8X4), scales=u_s[:, g], in_=u_bf[:, g].rearrange("p w j -> p (w j)")
+            )
+
+        gw = [keep.tile([P, S], U32, name=f"gw{a}", align_bytes=64) for a in range(A)]
+        gs = [keep.tile([P, S], U8, name=f"gs{a}", align_bytes=64) for a in range(A)]
+
+        def gather_scales(a):
+            nc.vector.tensor_copy(gs[a][:], tab_sc[:, a, :].bitcast(U8).indirect(offsets[:]))
+
+        def gather_words(a):
+            nc.vector.tensor_copy(gw[a][:], words[a][:].bitcast(U32).indirect(offsets[:]))
+
+        gather_scales(0)
+        gather_scales(1)
+        gather_words(0)
+
+        b_ps = psum.tile([P, 512], F32, name="b_ps", tag="bank7")
+        nc.tensor.transpose(b_ps[:, 0:P], b_row[:], ident[:])
+        nc.scalar.copy(b_col[:], b_ps[:, 0:1])
+        nc.tensor.transpose(b_ps[:, P : P + M], b_col[:].to_broadcast([P, P]), ident[:])
+        b_all = keep.tile([P, M], F32, name="b_all", align_bytes=64)
+        nc.scalar.copy(b_all[:], b_ps[:, P : P + M])
+
+        acc = [psum.tile([P, 512], F32, name=f"acc{t}", tag=f"bank{t}") for t in range(NT)]
+
+        def table_pass(a, t, start):
+            c = slice(P * t, P * (t + 1))
+            nc.tensor.matmul_mx(
+                out=acc[t][:, 0:M],
+                lhsT=gw[a][:, c].bitcast(FP8X4),
+                lhsT_scale=gs[a][:, c],
+                rhs=w4_w[:, a, :].bitcast(FP4X4),
+                rhs_scale=w4_s[:, a, :].bitcast(U8),
+                start=start,
+                stop=False,
+            )
+
+        for t in range(NT):
+            table_pass(0, t, True)
+
+        x_bf = [keep.tile([P, S, 4], BF16, name=f"x_bf{g}", align_bytes=64) for g in range(G)]
+        x_c = [keep.tile([P, S], U32, name=f"x_c{g}", align_bytes=64) for g in range(G)]
+        x_s = [keep.tile([P, S], U8, name=f"x_s{g}", align_bytes=64) for g in range(G)]
+
+        def x_copy(g, load0, w0, w1, sc):
+            dst = x_bf[g][:, w0:w1, :]
+            src = x_raw[g, load0][:, :, w0 - load0 : w1 - load0]
+            interleave(dst, src, 0, sc, "S")
+            interleave(dst, src, sc, w1 - w0, "V")
+
+        def x_quantize(g, w0, w1):
+            nc.vector.quantize_mx(
+                out=x_c[g][:, w0:w1].bitcast(FP8X4),
+                scales=x_s[g][:, w0:w1],
+                in_=x_bf[g][:, w0:w1, :].rearrange("p w j -> p (w j)"),
+            )
+
+        def x_group(g, load0, w0, w1, sc):
+            x_copy(g, load0, w0, w1, sc)
+            x_quantize(g, w0, w1)
+
+        def x_pass(g, t):
+            c = slice(P * t, P * (t + 1))
+            nc.tensor.matmul_mx(
+                out=acc[t][:, 0:M],
+                lhsT=x_c[g][:, c].bitcast(FP8X4),
+                lhsT_scale=x_s[g][:, c],
+                rhs=u_c[:, g].bitcast(FP8X4),
+                rhs_scale=u_s[:, g],
+                start=False,
+                stop=(g == G - 1),
+            )
+
+        for w0 in (0, 512):
+            x_group(0, 0, w0, w0 + 512, 512)
+            for t in range(w0 // P, w0 // P + 4):
+                x_pass(0, t)
+
+        gather_words(1)
+        for t in range(NT):
+            table_pass(1, t, False)
+
+        for w0 in (0, 512):
+            x_group(1, 0, w0, w0 + 512, 272)
+            for t in range(w0 // P, w0 // P + 4):
+                x_pass(1, t)
+
+        y = keep.tile([P, NT, M], F32, name="y", align_bytes=64)
+        o = keep.tile([P, NT, M], F32, name="o", align_bytes=64)
+
+        def finish(t0, t1):
+            for t in range(t0, t1):
+                nc.vector.tensor_tensor(y[:, t], acc[t][:, 0:M], b_all[:], ADD)
+            nc.scalar.activation(o[:, t0:t1], y[:, t0:t1], SILU)
+            nc.sync.dma_start(
+                out=out[P * t0 : P * t1, :].rearrange("(t p) n -> p t n", p=P), in_=o[:, t0:t1]
+            )
+
+        for w0 in (0, 256, 512):
+            x_copy(2, 0, w0, w0 + 256, 136)
+        for w0 in (0, 256, 512):
+            x_quantize(2, w0, w0 + 256)
+            for t in (w0 // P, w0 // P + 1):
+                x_pass(2, t)
+        for t in (0, 2):
+            finish(t, t + 2)
+        x_copy(2, 768, 768, 896, 64)
+        x_copy(2, 768, 896, 1024, 64)
+        finish(4, 6)
+        x_quantize(2, 768, 896)
+        x_quantize(2, 896, 1024)
+        for t in range(6, 8):
+            x_pass(2, t)
+            finish(t, t + 1)

@@ -22,6 +22,8 @@ KP = 512
 A = K // KP
 G = L // KP
 NT = S // P
+BANKS = ((0, 2), (2, 4), (4, 5), (5, 6), (6, 7), (7, 8))
+LAST_LOADS = ((0, 640), (640, 1024))
 
 
 def tile_list_tabx_tm_silu_kernel(tc, tab, w4_words, w4_scales, x, u, b, offs, out):
@@ -33,7 +35,9 @@ def tile_list_tabx_tm_silu_kernel(tc, tab, w4_words, w4_scales, x, u, b, offs, o
 
         offsets = keep.tile([P, S // 16], U16, name="offsets")
         u_raw = keep.tile([P, G, 4, M], F32, name="u_raw", align_bytes=64)
-        tab_sc = keep.tile([P, A, T // 4], I32, name="tab_sc", align_bytes=64)
+        tab_sc = keep.tile([P, T // 4], I32, name="tab_sc", align_bytes=64)
+        picked_sc = keep.tile([P, S], U8, name="picked_sc", align_bytes=64)
+        gs = keep.tile([P, A, S // 4], I32, name="gs", align_bytes=64)
         words = [keep.tile([P, T], I32, name=f"words{a}", align_bytes=64) for a in range(A)]
         w4_w = keep.tile([P, A, 2 * M], U8, name="w4_w", align_bytes=64)
         w4_s = keep.tile([P, A, M // 4], I32, name="w4_s", align_bytes=64)
@@ -46,16 +50,12 @@ def tile_list_tabx_tm_silu_kernel(tc, tab, w4_words, w4_scales, x, u, b, offs, o
         tab_i = tab.bitcast(I32)
         nc.vector.memset(tab_sc[:], 0)
         nc.vector.memset(w4_s[:], 0)
+        nc.vector.memset(gs[:], 0)
         nc.gpsimd.memset(warm[:], 0.0)
         nc.gpsimd.memset(b_row[:], 0.0)
 
         def load_words(a):
             nc.sync.dma_start(out=words[a][:], in_=tab_i[a, 0 : 128 * T].rearrange("(p t) -> p t", p=P))
-
-        def load_scales(tile, rows):
-            view = rows.rearrange("a (q r) n -> r q a n", r=4)
-            for r in range(4):
-                nc.sync.dma_start(out=tile[r:P:32], in_=view[r])
 
         x_raw = {}
 
@@ -65,17 +65,26 @@ def tile_list_tabx_tm_silu_kernel(tc, tab, w4_words, w4_scales, x, u, b, offs, o
             x_raw[g, w0] = t
 
         load_words(0)
+        nc.sync.dma_start(
+            out=tab_sc[0:P:4], in_=tab_i[:, 128 * T : 132 * T].rearrange("a (i t) -> i a t", i=16)
+        )
         nc.sync.dma_start(offsets[:], offs)
-        nc.sync.dma_start(out=b_row[0:1, :], in_=b.rearrange("(o n) -> o n", o=1))
-        load_scales(tab_sc, tab_i[:, 128 * T : 132 * T].rearrange("a (q t) -> a q t", q=16))
-        nc.sync.dma_start(out=u_raw[:], in_=u.rearrange("(g p j) n -> p g j n", p=P, j=4))
-        load_x(0, 0, S)
-        nc.sync.dma_start(out=w4_w[:].bitcast(I32), in_=w4_words.bitcast(I32).rearrange("a p n -> p a n"))
-        load_scales(w4_s, w4_scales.bitcast(I32))
+        w4_rows = w4_scales.bitcast(I32).rearrange("a (q r) n -> r q a n", r=4)
+        for r in range(4):
+            nc.sync.dma_start(out=w4_s[r:P:32], in_=w4_rows[r])
         load_words(1)
+        nc.sync.dma_start(out=u_raw[:], in_=u.rearrange("(g p j) n -> p g j n", p=P, j=4))
+        nc.sync.dma_start(out=w4_w[:].bitcast(I32), in_=w4_words.bitcast(I32).rearrange("a p n -> p a n"))
+        nc.sync.dma_start(out=b_row[0:1, :], in_=b.rearrange("(o n) -> o n", o=1))
+        load_x(0, 0, S)
+        nc.vector.tensor_copy(picked_sc[:], tab_sc[:].bitcast(U8).indirect(offsets[:]))
+        for q in range(4):
+            nc.sync.dma_start(
+                out=gs[32 * q : 32 * q + 4], in_=picked_sc[:].bitcast(I32)[32 * q : 32 * q + 32 : 4]
+            )
         load_x(1, 0, S)
-        load_x(2, 0, 768)
-        load_x(2, 768, 1024)
+        for w0, w1 in LAST_LOADS:
+            load_x(2, w0, w1)
 
         make_identity(nc, ident[:])
         nc.scalar.activation(warm2[:], warm[:], SILU)
@@ -92,49 +101,44 @@ def tile_list_tabx_tm_silu_kernel(tc, tab, w4_words, w4_scales, x, u, b, offs, o
         u_bf = keep.tile([P, G, M, 4], BF16, name="u_bf", align_bytes=64)
         u_c = keep.tile([P, G, M], U32, name="u_c", align_bytes=64)
         u_s = keep.tile([P, G, M], U8, name="u_s", align_bytes=64)
-        for g in range(G):
-            interleave(u_bf[:, g], u_raw[:, g], 0, M, "S")
-        for g in range(G):
-            nc.vector.quantize_mx(
-                out=u_c[:, g].bitcast(FP8X4), scales=u_s[:, g], in_=u_bf[:, g].rearrange("p w j -> p (w j)")
-            )
 
         gw = [keep.tile([P, S], U32, name=f"gw{a}", align_bytes=64) for a in range(A)]
-        gs = [keep.tile([P, S], U8, name=f"gs{a}", align_bytes=64) for a in range(A)]
 
-        def gather_scales(a):
-            nc.vector.tensor_copy(gs[a][:], tab_sc[:, a, :].bitcast(U8).indirect(offsets[:]))
+        def gather_words(a, w0, w1):
+            nc.vector.tensor_copy(
+                gw[a][:, w0:w1], words[a][:].bitcast(U32).indirect(offsets[:, w0 // 16 : w1 // 16])
+            )
 
-        def gather_words(a):
-            nc.vector.tensor_copy(gw[a][:], words[a][:].bitcast(U32).indirect(offsets[:]))
-
-        gather_scales(0)
-        gather_scales(1)
-        gather_words(0)
+        gather_words(0, 0, S)
+        gather_words(1, 0, S)
 
         b_ps = psum.tile([P, 512], F32, name="b_ps", tag="bank7")
         nc.tensor.transpose(b_ps[:, 0:P], b_row[:], ident[:])
         nc.scalar.copy(b_col[:], b_ps[:, 0:1])
-        nc.tensor.transpose(b_ps[:, P : P + M], b_col[:].to_broadcast([P, P]), ident[:])
-        b_all = keep.tile([P, M], F32, name="b_all", align_bytes=64)
-        nc.scalar.copy(b_all[:], b_ps[:, P : P + M])
+        for s in range(2):
+            nc.tensor.transpose(b_ps[:, P + M * s : P + M * (s + 1)], b_col[:].to_broadcast([P, P]), ident[:])
+        b_all = keep.tile([P, 2 * M], F32, name="b_all", align_bytes=64)
+        nc.scalar.copy(b_all[:], b_ps[:, P : P + 2 * M])
 
-        acc = [psum.tile([P, 512], F32, name=f"acc{t}", tag=f"bank{t}") for t in range(NT)]
+        acc = [psum.tile([P, 512], F32, name=f"acc{i}", tag=f"bank{i}") for i in range(len(BANKS))]
+        where = {t: (i, t - t0) for i, (t0, t1) in enumerate(BANKS) for t in range(t0, t1)}
 
-        def table_pass(a, t, start):
+        def acc_of(t):
+            i, s = where[t]
+            return acc[i][:, M * s : M * (s + 1)]
+
+        def table_pass(a, t):
             c = slice(P * t, P * (t + 1))
             nc.tensor.matmul_mx(
-                out=acc[t][:, 0:M],
+                out=acc_of(t),
                 lhsT=gw[a][:, c].bitcast(FP8X4),
-                lhsT_scale=gs[a][:, c],
+                lhsT_scale=gs[:, a, :].bitcast(U8)[:, c],
                 rhs=w4_w[:, a, :].bitcast(FP4X4),
                 rhs_scale=w4_s[:, a, :].bitcast(U8),
-                start=start,
+                start=False,
                 stop=False,
             )
 
-        for t in range(NT):
-            table_pass(0, t, True)
 
         x_bf = [keep.tile([P, S, 4], BF16, name=f"x_bf{g}", align_bytes=64) for g in range(G)]
         x_c = [keep.tile([P, S], U32, name=f"x_c{g}", align_bytes=64) for g in range(G)]
@@ -153,60 +157,71 @@ def tile_list_tabx_tm_silu_kernel(tc, tab, w4_words, w4_scales, x, u, b, offs, o
                 in_=x_bf[g][:, w0:w1, :].rearrange("p w j -> p (w j)"),
             )
 
-        def x_group(g, load0, w0, w1, sc):
-            x_copy(g, load0, w0, w1, sc)
-            x_quantize(g, w0, w1)
-
         def x_pass(g, t):
             c = slice(P * t, P * (t + 1))
             nc.tensor.matmul_mx(
-                out=acc[t][:, 0:M],
+                out=acc_of(t),
                 lhsT=x_c[g][:, c].bitcast(FP8X4),
                 lhsT_scale=x_s[g][:, c],
                 rhs=u_c[:, g].bitcast(FP8X4),
                 rhs_scale=u_s[:, g],
-                start=False,
-                stop=(g == G - 1),
+                start=(g == 0 and where[t][1] == 0),
+                stop=(g == G - 1 and t + 1 == BANKS[where[t][0]][1]),
             )
 
-        for w0 in (0, 512):
-            x_group(0, 0, w0, w0 + 512, 512)
-            for t in range(w0 // P, w0 // P + 4):
-                x_pass(0, t)
+        for g in range(G):
+            interleave(u_bf[:, g], u_raw[:, g], 0, M, "S")
+        for g0, g1 in ((0, 2), (2, 3)):
+            nc.vector.quantize_mx(
+                out=u_c[:, g0:g1].rearrange("p g w -> p (g w)").bitcast(FP8X4),
+                scales=u_s[:, g0:g1].rearrange("p g w -> p (g w)"),
+                in_=u_bf[:, g0:g1].rearrange("p g w j -> p (g w j)"),
+            )
 
-        gather_words(1)
-        for t in range(NT):
-            table_pass(1, t, False)
+        for g in (0, 1):
+            for w0 in (0, 512):
+                x_copy(g, 0, w0, w0 + 512, 288)
+            for w0 in (0, 512):
+                x_quantize(g, w0, w0 + 512)
+            for t in range(NT):
+                x_pass(g, t)
+            if g == 0:
+                for a in range(A):
+                    for t in range(NT):
+                        table_pass(a, t)
 
-        for w0 in (0, 512):
-            x_group(1, 0, w0, w0 + 512, 272)
-            for t in range(w0 // P, w0 // P + 4):
-                x_pass(1, t)
-
-        y = keep.tile([P, NT, M], F32, name="y", align_bytes=64)
+        y = keep.tile([P, NT * M], F32, name="y", align_bytes=64)
         o = keep.tile([P, NT, M], F32, name="o", align_bytes=64)
 
-        def finish(t0, t1):
-            for t in range(t0, t1):
-                nc.vector.tensor_tensor(y[:, t], acc[t][:, 0:M], b_all[:], ADD)
-            nc.scalar.activation(o[:, t0:t1], y[:, t0:t1], SILU)
+        def finish(i):
+            t0, t1 = BANKS[i]
+            n = M * (t1 - t0)
+            nc.vector.tensor_tensor(y[:, M * t0 : M * t1], acc[i][:, 0:n], b_all[:, 0:n], ADD)
+            nc.scalar.activation(o[:, t0:t1].rearrange("p t n -> p (t n)"), y[:, M * t0 : M * t1], SILU)
             nc.sync.dma_start(
                 out=out[P * t0 : P * t1, :].rearrange("(t p) n -> p t n", p=P), in_=o[:, t0:t1]
             )
 
-        for w0 in (0, 256, 512):
-            x_copy(2, 0, w0, w0 + 256, 136)
-        for w0 in (0, 256, 512):
-            x_quantize(2, w0, w0 + 256)
-            for t in (w0 // P, w0 // P + 1):
+        def multiply(w0, w1):
+            x_quantize(2, w0, w1)
+            for t in range(w0 // P, w1 // P):
                 x_pass(2, t)
-        for t in (0, 2):
-            finish(t, t + 2)
-        x_copy(2, 768, 768, 896, 64)
-        x_copy(2, 768, 896, 1024, 64)
-        finish(4, 6)
-        x_quantize(2, 768, 896)
-        x_quantize(2, 896, 1024)
-        for t in range(6, 8):
-            x_pass(2, t)
-            finish(t, t + 1)
+
+        x_copy(2, 0, 0, 256, 160)
+        x_copy(2, 0, 256, 512, 160)
+        multiply(0, 256)
+        x_copy(2, 0, 512, 640, 80)
+        multiply(256, 512)
+        multiply(512, 640)
+        finish(0)
+        x_copy(2, 640, 640, 768, 80)
+        x_copy(2, 640, 768, 896, 80)
+        finish(1)
+        multiply(640, 768)
+        x_copy(2, 640, 896, 1024, 64)
+        finish(2)
+        multiply(768, 896)
+        multiply(896, 1024)
+        finish(3)
+        finish(4)
+        finish(5)

@@ -22,8 +22,8 @@ KP = 512
 A = K // KP
 G = L // KP
 NT = S // P
-BANKS = ((0, 2), (2, 4), (4, 5), (5, 6), (6, 7), (7, 8))
-LAST_LOADS = ((0, 640), (640, 1024))
+BANKS = ((0, 2), (2, 4), (4, 6), (6, 7), (7, 8))
+WIDE = 2
 
 
 def tile_list_tabx_tm_silu_kernel(tc, tab, w4_words, w4_scales, x, u, b, offs, out):
@@ -37,10 +37,10 @@ def tile_list_tabx_tm_silu_kernel(tc, tab, w4_words, w4_scales, x, u, b, offs, o
         u_raw = keep.tile([P, G, 4, M], F32, name="u_raw", align_bytes=64)
         tab_sc = keep.tile([P, T // 4], I32, name="tab_sc", align_bytes=64)
         picked_sc = keep.tile([P, S], U8, name="picked_sc", align_bytes=64)
-        gs = keep.tile([P, A, S // 4], I32, name="gs", align_bytes=64)
-        words = [keep.tile([P, T], I32, name=f"words{a}", align_bytes=64) for a in range(A)]
+        spread = keep.tile([P, (S + M) // 4], I32, name="spread", align_bytes=64)
+        planes = keep.tile([P, A, (S + M) // 4], I32, name="planes", align_bytes=64)
+        words = [keep.tile([P, T], I32, name=f"words{a}", align_bytes=64)[:] for a in range(A)]
         w4_w = keep.tile([P, A, 2 * M], U8, name="w4_w", align_bytes=64)
-        w4_s = keep.tile([P, A, M // 4], I32, name="w4_s", align_bytes=64)
         b_row = keep.tile([P, M], F32, name="b_row", align_bytes=64)
         b_col = keep.tile([P, 1], F32, name="b_col", align_bytes=64)
         ident = keep.tile([P, P], F32, name="ident", align_bytes=64)
@@ -49,42 +49,61 @@ def tile_list_tabx_tm_silu_kernel(tc, tab, w4_words, w4_scales, x, u, b, offs, o
 
         tab_i = tab.bitcast(I32)
         nc.vector.memset(tab_sc[:], 0)
-        nc.vector.memset(w4_s[:], 0)
-        nc.vector.memset(gs[:], 0)
+        nc.vector.memset(planes[:], 0)
         nc.gpsimd.memset(warm[:], 0.0)
         nc.gpsimd.memset(b_row[:], 0.0)
 
         def load_words(a):
-            nc.sync.dma_start(out=words[a][:], in_=tab_i[a, 0 : 128 * T].rearrange("(p t) -> p t", p=P))
+            nc.sync.dma_start(out=words[a], in_=tab_i[a, 0 : 128 * T].rearrange("(p t) -> p t", p=P))
+
+        def load_u(g0, g1):
+            rows = u[KP * g0 : KP * g1, :].rearrange("(g p j) n -> p g j n", p=P, j=4)
+            nc.sync.dma_start(out=u_raw[:, g0:g1], in_=rows)
 
         x_raw = {}
 
         def load_x(g, w0, w1):
-            t = keep.tile([P, 4, w1 - w0], F32, name=f"x_raw{g}_{w0}", align_bytes=64)
+            t = keep.tile([P, 4, w1 - w0], F32, name=f"x_raw{g}_{w0}", tag=f"x_raw{g}_{w0}", align_bytes=64)
             nc.sync.dma_start(out=t[:], in_=x[KP * g : KP * (g + 1), w0:w1].rearrange("(p j) w -> p j w", j=4))
-            x_raw[g, w0] = t
+            for w in range(w0, w1):
+                x_raw[g, w] = (t, w0)
+
+        def load_scales():
+            nc.sync.dma_start(
+                out=tab_sc[0:P:4], in_=tab_i[:, 128 * T : 132 * T].rearrange("a (i t) -> i a t", i=16)
+            )
+
+        def load_w4_scales():
+            nc.sync.dma_start(
+                out=spread[0:P:4, S // 4 :], in_=w4_scales.bitcast(I32).rearrange("a i n -> i a n")
+            )
+
+        def load_w4():
+            nc.sync.dma_start(out=w4_w[:].bitcast(I32), in_=w4_words.bitcast(I32).rearrange("a p n -> p a n"))
+
+        def load_b():
+            nc.sync.dma_start(out=b_row[0:1, :], in_=b.rearrange("(o n) -> o n", o=1))
+
+        def place_scales():
+            nc.vector.tensor_copy(picked_sc[:], tab_sc[:].bitcast(U8).indirect(offsets[:]))
+            nc.vector.tensor_copy(spread[:, 0 : S // 4], picked_sc[:].bitcast(I32))
+            for q in range(4):
+                nc.sync.dma_start(out=planes[32 * q : 32 * q + 4], in_=spread[32 * q : 32 * q + 32 : 4])
 
         load_words(0)
-        nc.sync.dma_start(
-            out=tab_sc[0:P:4], in_=tab_i[:, 128 * T : 132 * T].rearrange("a (i t) -> i a t", i=16)
-        )
+        load_scales()
         nc.sync.dma_start(offsets[:], offs)
-        w4_rows = w4_scales.bitcast(I32).rearrange("a (q r) n -> r q a n", r=4)
-        for r in range(4):
-            nc.sync.dma_start(out=w4_s[r:P:32], in_=w4_rows[r])
+        load_w4_scales()
         load_words(1)
-        nc.sync.dma_start(out=u_raw[:], in_=u.rearrange("(g p j) n -> p g j n", p=P, j=4))
-        nc.sync.dma_start(out=w4_w[:].bitcast(I32), in_=w4_words.bitcast(I32).rearrange("a p n -> p a n"))
-        nc.sync.dma_start(out=b_row[0:1, :], in_=b.rearrange("(o n) -> o n", o=1))
+        load_u(0, 2)
+        load_w4()
+        load_b()
         load_x(0, 0, S)
-        nc.vector.tensor_copy(picked_sc[:], tab_sc[:].bitcast(U8).indirect(offsets[:]))
-        for q in range(4):
-            nc.sync.dma_start(
-                out=gs[32 * q : 32 * q + 4], in_=picked_sc[:].bitcast(I32)[32 * q : 32 * q + 32 : 4]
-            )
+        place_scales()
         load_x(1, 0, S)
-        for w0, w1 in LAST_LOADS:
-            load_x(2, w0, w1)
+        load_u(2, 3)
+        for w0 in range(0, S, 256):
+            load_x(2, w0, w0 + 256)
 
         make_identity(nc, ident[:])
         nc.scalar.activation(warm2[:], warm[:], SILU)
@@ -102,126 +121,128 @@ def tile_list_tabx_tm_silu_kernel(tc, tab, w4_words, w4_scales, x, u, b, offs, o
         u_c = keep.tile([P, G, M], U32, name="u_c", align_bytes=64)
         u_s = keep.tile([P, G, M], U8, name="u_s", align_bytes=64)
 
-        gw = [keep.tile([P, S], U32, name=f"gw{a}", align_bytes=64) for a in range(A)]
-
-        def gather_words(a, w0, w1):
-            nc.vector.tensor_copy(
-                gw[a][:, w0:w1], words[a][:].bitcast(U32).indirect(offsets[:, w0 // 16 : w1 // 16])
-            )
-
-        gather_words(0, 0, S)
-        gather_words(1, 0, S)
-
-        b_ps = psum.tile([P, 512], F32, name="b_ps", tag="bank7")
-        nc.tensor.transpose(b_ps[:, 0:P], b_row[:], ident[:])
-        nc.scalar.copy(b_col[:], b_ps[:, 0:1])
-        for s in range(2):
-            nc.tensor.transpose(b_ps[:, P + M * s : P + M * (s + 1)], b_col[:].to_broadcast([P, P]), ident[:])
-        b_all = keep.tile([P, 2 * M], F32, name="b_all", align_bytes=64)
-        nc.scalar.copy(b_all[:], b_ps[:, P : P + 2 * M])
-
-        acc = [psum.tile([P, 512], F32, name=f"acc{i}", tag=f"bank{i}") for i in range(len(BANKS))]
-        where = {t: (i, t - t0) for i, (t0, t1) in enumerate(BANKS) for t in range(t0, t1)}
-
-        def acc_of(t):
-            i, s = where[t]
-            return acc[i][:, M * s : M * (s + 1)]
-
-        def table_pass(a, t):
-            c = slice(P * t, P * (t + 1))
-            nc.tensor.matmul_mx(
-                out=acc_of(t),
-                lhsT=gw[a][:, c].bitcast(FP8X4),
-                lhsT_scale=gs[:, a, :].bitcast(U8)[:, c],
-                rhs=w4_w[:, a, :].bitcast(FP4X4),
-                rhs_scale=w4_s[:, a, :].bitcast(U8),
-                start=False,
-                stop=False,
-            )
-
-
-        x_bf = [keep.tile([P, S, 4], BF16, name=f"x_bf{g}", align_bytes=64) for g in range(G)]
-        x_c = [keep.tile([P, S], U32, name=f"x_c{g}", align_bytes=64) for g in range(G)]
-        x_s = [keep.tile([P, S], U8, name=f"x_s{g}", align_bytes=64) for g in range(G)]
-
-        def x_copy(g, load0, w0, w1, sc):
-            dst = x_bf[g][:, w0:w1, :]
-            src = x_raw[g, load0][:, :, w0 - load0 : w1 - load0]
-            interleave(dst, src, 0, sc, "S")
-            interleave(dst, src, sc, w1 - w0, "V")
-
-        def x_quantize(g, w0, w1):
-            nc.vector.quantize_mx(
-                out=x_c[g][:, w0:w1].bitcast(FP8X4),
-                scales=x_s[g][:, w0:w1],
-                in_=x_bf[g][:, w0:w1, :].rearrange("p w j -> p (w j)"),
-            )
-
-        def x_pass(g, t):
-            c = slice(P * t, P * (t + 1))
-            nc.tensor.matmul_mx(
-                out=acc_of(t),
-                lhsT=x_c[g][:, c].bitcast(FP8X4),
-                lhsT_scale=x_s[g][:, c],
-                rhs=u_c[:, g].bitcast(FP8X4),
-                rhs_scale=u_s[:, g],
-                start=(g == 0 and where[t][1] == 0),
-                stop=(g == G - 1 and t + 1 == BANKS[where[t][0]][1]),
-            )
-
-        for g in range(G):
-            interleave(u_bf[:, g], u_raw[:, g], 0, M, "S")
-        for g0, g1 in ((0, 2), (2, 3)):
+        def u_quantize(g0, g1, by):
+            for g in range(g0, g1):
+                interleave(u_bf[:, g], u_raw[:, g], 0, M, by)
             nc.vector.quantize_mx(
                 out=u_c[:, g0:g1].rearrange("p g w -> p (g w)").bitcast(FP8X4),
                 scales=u_s[:, g0:g1].rearrange("p g w -> p (g w)"),
                 in_=u_bf[:, g0:g1].rearrange("p g w j -> p (g w j)"),
             )
 
-        for g in (0, 1):
-            for w0 in (0, 512):
-                x_copy(g, 0, w0, w0 + 512, 288)
-            for w0 in (0, 512):
-                x_quantize(g, w0, w0 + 512)
-            for t in range(NT):
-                x_pass(g, t)
-            if g == 0:
-                for a in range(A):
-                    for t in range(NT):
-                        table_pass(a, t)
+        gw = [keep.tile([P, S], U32, name=f"gw{a}", align_bytes=64) for a in range(A)]
 
-        y = keep.tile([P, NT * M], F32, name="y", align_bytes=64)
-        o = keep.tile([P, NT, M], F32, name="o", align_bytes=64)
-
-        def finish(i):
-            t0, t1 = BANKS[i]
-            n = M * (t1 - t0)
-            nc.vector.tensor_tensor(y[:, M * t0 : M * t1], acc[i][:, 0:n], b_all[:, 0:n], ADD)
-            nc.scalar.activation(o[:, t0:t1].rearrange("p t n -> p (t n)"), y[:, M * t0 : M * t1], SILU)
-            nc.sync.dma_start(
-                out=out[P * t0 : P * t1, :].rearrange("(t p) n -> p t n", p=P), in_=o[:, t0:t1]
+        def gather_words(a, w0, w1):
+            nc.vector.tensor_copy(
+                gw[a][:, w0:w1], words[a].bitcast(U32).indirect(offsets[:, w0 // 16 : w1 // 16])
             )
 
-        def multiply(w0, w1):
-            x_quantize(2, w0, w1)
-            for t in range(w0 // P, w1 // P):
-                x_pass(2, t)
+        def bias():
+            b_ps = psum.tile([P, 512], F32, name="b_ps", tag="bank7")
+            nc.tensor.transpose(b_ps[:, 0:P], b_row[:], ident[:])
+            nc.scalar.copy(b_col[:], b_ps[:, 0:1])
+            for s in range(WIDE):
+                nc.tensor.transpose(b_ps[:, P + M * s : P + M * (s + 1)], b_col[:].to_broadcast([P, P]), ident[:])
+            nc.scalar.copy(b_all[:], b_ps[:, P : P + WIDE * M])
 
-        x_copy(2, 0, 0, 256, 160)
-        x_copy(2, 0, 256, 512, 160)
-        multiply(0, 256)
-        x_copy(2, 0, 512, 640, 80)
-        multiply(256, 512)
-        multiply(512, 640)
-        finish(0)
-        x_copy(2, 640, 640, 768, 80)
-        x_copy(2, 640, 768, 896, 80)
-        finish(1)
-        multiply(640, 768)
-        x_copy(2, 640, 896, 1024, 64)
-        finish(2)
-        multiply(768, 896)
-        multiply(896, 1024)
-        finish(3)
-        finish(4)
-        finish(5)
+        b_all = keep.tile([P, WIDE * M], F32, name="b_all", align_bytes=64)
+        acc = [psum.tile([P, 512], F32, name=f"acc{i}", tag=f"bank{i}") for i in range(len(BANKS))]
+        where = {t: (i, t - t0) for i, (t0, t1) in enumerate(BANKS) for t in range(t0, t1)}
+        passes_done = {i: [] for i in range(len(BANKS))}
+
+        def mx_pass(t, codes, scales, w_codes, w_scales):
+            i, s = where[t]
+            c = slice(P * t, P * (t + 1))
+            done = passes_done[i]
+            done.append(t)
+            nc.tensor.matmul_mx(
+                out=acc[i][:, M * s : M * (s + 1)],
+                lhsT=codes[:, c].bitcast(FP8X4),
+                lhsT_scale=scales[:, c],
+                rhs=w_codes,
+                rhs_scale=w_scales,
+                start=(len(done) == 1),
+                stop=(len(done) == (A + G) * (BANKS[i][1] - BANKS[i][0])),
+            )
+
+        def table_passes(a, w0, w1):
+            plane = planes[:, a, :].bitcast(U8)
+            for t in range(w0 // P, w1 // P):
+                mx_pass(t, gw[a], plane, w4_w[:, a, :].bitcast(FP4X4), plane[:, S : S + M])
+
+        x_bf = {}
+        x_c = [keep.tile([P, S], U32, name=f"x_c{g}", align_bytes=64) for g in range(G)]
+        x_s = [keep.tile([P, S], U8, name=f"x_s{g}", align_bytes=64) for g in range(G)]
+
+        def x_copy(g, w0, w1, sc):
+            raw, load0 = x_raw[g, w0]
+            dst = keep.tile([P, w1 - w0, 4], BF16, name=f"x_bf{g}_{w0}", tag=f"x_bf{g}_{w0}", align_bytes=64)
+            x_bf[g, w0] = dst
+            src = raw[:, :, w0 - load0 : w1 - load0]
+            interleave(dst, src, 0, sc, "S")
+            interleave(dst, src, sc, w1 - w0, "V")
+
+        def quantize(g, w0, w1):
+            nc.vector.quantize_mx(
+                out=x_c[g][:, w0:w1].bitcast(FP8X4),
+                scales=x_s[g][:, w0:w1],
+                in_=x_bf[g, w0][:].rearrange("p w j -> p (w j)"),
+            )
+
+        def x_passes(g, w0, w1):
+            for t in range(w0 // P, w1 // P):
+                mx_pass(t, x_c[g], x_s[g], u_c[:, g].bitcast(FP8X4), u_s[:, g])
+
+        def multiply(g, w0, w1):
+            quantize(g, w0, w1)
+            x_passes(g, w0, w1)
+
+
+        def finish(i, y, o, queue):
+            t0, t1 = BANKS[i]
+            n = M * (t1 - t0)
+            nc.vector.tensor_tensor(
+                y,
+                acc[i][:, 0:n].rearrange("p (j c) -> p j c", j=4),
+                b_all[:, 0:n].rearrange("p (j c) -> p j c", j=4),
+                ADD,
+            )
+            nc.scalar.activation(
+                o.rearrange("p t (h c) -> p t h c", c=n // 4), y.rearrange("p (t h) c -> p t h c", t=t1 - t0), SILU
+            )
+            queue.dma_start(
+                out=out[P * t0 : P * t1, :].rearrange("(t p) n -> p t n", p=P), in_=o
+            )
+
+        gather_words(0, 0, S)
+        gather_words(1, 0, S)
+        u_quantize(0, 2, "S")
+        bias()
+        x_copy(0, 0, 512, 264)
+        x_copy(0, 512, S, 264)
+        multiply(0, 0, 512)
+        table_passes(0, 0, S)
+        multiply(0, 512, S)
+        table_passes(1, 0, S)
+        x_copy(1, 0, 512, 264)
+        x_copy(1, 512, S, 264)
+        multiply(1, 0, 512)
+        multiply(1, 512, S)
+        u_quantize(2, 3, "S")
+        for i in range(3):
+            w0 = 256 * i
+            x_copy(2, w0, w0 + 256, 136)
+            if i > 0:
+                raw = x_raw[2, w0][0]
+                finish(i - 1, raw[:, :, 136:200], raw[:, 0:2, 0:M], nc.sync)
+            multiply(2, w0, w0 + 256)
+        x_copy(2, 768, 896, 128)
+        x_copy(2, 896, S, 0)
+        raw = x_raw[2, 768][0]
+        finish(2, raw[:, :, 128:192], raw[:, 0:2, 0:M], nc.sync)
+        multiply(2, 896, S)
+        multiply(2, 768, 896)
+        y = keep.tile([P, 2, 4, M // 4], F32, name="y", align_bytes=64)
+        o = keep.tile([P, 2, M], F32, name="o", align_bytes=64)
+        finish(4, y[:, 1], o[:, 1:2], nc.sync)
+        finish(3, y[:, 0], o[:, 0:1], nc.scalar)

@@ -94,13 +94,13 @@ def tile_list_tabx_tm_silu_kernel(tc, tab, w4_words, w4_scales, x, u, b, offs, o
         load_scales()
         nc.sync.dma_start(offsets[:], offs)
         load_w4_scales()
-        load_words(1)
         load_u(0, 2)
         load_w4()
         load_b()
         load_x(0, 0, S)
-        place_scales()
         load_x(1, 0, S)
+        place_scales()
+        load_words(1)
         load_u(2, 3)
         for w0 in range(0, S, 256):
             load_x(2, w0, w0 + 256)
@@ -215,26 +215,27 @@ def tile_list_tabx_tm_silu_kernel(tc, tab, w4_words, w4_scales, x, u, b, offs, o
             )
 
         gather_words(0, 0, S)
-        gather_words(1, 0, S)
         u_quantize(0, 2, "S")
         bias()
         x_copy(0, 0, 512, 264)
         x_copy(0, 512, S, 264)
         multiply(0, 0, 512)
-        table_passes(0, 0, S)
         multiply(0, 512, S)
-        table_passes(1, 0, S)
         x_copy(1, 0, 512, 264)
         x_copy(1, 512, S, 264)
         multiply(1, 0, 512)
         multiply(1, 512, S)
+        table_passes(0, 0, S)
+        for w0 in range(0, S, 256):
+            gather_words(1, w0, w0 + 256)
+            table_passes(1, w0, w0 + 256)
         u_quantize(2, 3, "S")
-        for i in range(3):
+        for i, share in enumerate((256, 192, 128)):
             w0 = 256 * i
-            x_copy(2, w0, w0 + 256, 136)
+            x_copy(2, w0, w0 + 256, share)
             if i > 0:
                 raw = x_raw[2, w0][0]
-                finish(i - 1, raw[:, :, 136:200], raw[:, 0:2, 0:M], nc.sync)
+                finish(i - 1, raw[:, :, 192:256], raw[:, 0:2, 0:M], nc.sync)
             multiply(2, w0, w0 + 256)
         x_copy(2, 768, 896, 128)
         x_copy(2, 896, S, 0)

@@ -94,12 +94,12 @@ def tile_list_tabx_tm_silu_kernel(tc, tab, w4_words, w4_scales, x, u, b, offs, o
         load_scales()
         nc.sync.dma_start(offsets[:], offs)
         load_w4_scales()
-        load_u(0, 2)
         load_w4()
         load_b()
         load_x(0, 0, S)
         load_x(1, 0, S)
         place_scales()
+        load_u(0, 2)
         load_words(1)
         load_u(2, 3)
         for w0 in range(0, S, 256):
@@ -215,35 +215,32 @@ def tile_list_tabx_tm_silu_kernel(tc, tab, w4_words, w4_scales, x, u, b, offs, o
             )
 
         gather_words(0, 0, S)
-        u_quantize(0, 2, "S")
         bias()
-        x_copy(0, 0, 512, 264)
-        x_copy(0, 512, S, 264)
-        multiply(0, 0, 512)
-        multiply(0, 512, S)
-        x_copy(1, 0, 512, 264)
-        x_copy(1, 512, S, 264)
-        multiply(1, 0, 512)
-        multiply(1, 512, S)
+        for g in range(2):
+            x_copy(g, 0, 512, 216)
+            x_copy(g, 512, S, 216)
+            quantize(g, 0, 512)
+            quantize(g, 512, S)
         table_passes(0, 0, S)
-        for w0 in range(0, S, 256):
-            gather_words(1, w0, w0 + 256)
-            table_passes(1, w0, w0 + 256)
+        u_quantize(0, 2, "S")
+        x_passes(0, 0, S)
+        x_passes(1, 0, S)
+        gather_words(1, 0, S)
+        table_passes(1, 0, S)
         u_quantize(2, 3, "S")
-        for i, share in enumerate((256, 192, 128)):
+        y = keep.tile([P, 2, 4, WIDE * M // 4], F32, name="y", align_bytes=64)
+        o = keep.tile([P, 4, WIDE, M], F32, name="o", align_bytes=64)
+        for i, share in enumerate((256, 160, 144)):
             w0 = 256 * i
             x_copy(2, w0, w0 + 256, share)
-            if i > 0:
-                raw = x_raw[2, w0][0]
-                finish(i - 1, raw[:, :, 192:256], raw[:, 0:2, 0:M], nc.sync)
+            if i > 1:
+                finish(i - 2, x_raw[2, w0][0][:, :, 192:256], o[:, i - 2], nc.sync)
             multiply(2, w0, w0 + 256)
         x_copy(2, 768, 896, 128)
         x_copy(2, 896, S, 0)
-        raw = x_raw[2, 768][0]
-        finish(2, raw[:, :, 128:192], raw[:, 0:2, 0:M], nc.sync)
-        multiply(2, 896, S)
+        finish(1, x_raw[2, 768][0][:, :, 192:256], o[:, 1], nc.sync)
         multiply(2, 768, 896)
-        y = keep.tile([P, 2, 4, M // 4], F32, name="y", align_bytes=64)
-        o = keep.tile([P, 2, M], F32, name="o", align_bytes=64)
-        finish(4, y[:, 1], o[:, 1:2], nc.sync)
-        finish(3, y[:, 0], o[:, 0:1], nc.scalar)
+        multiply(2, 896, S)
+        finish(2, x_bf[2, 896][:].rearrange("p w j -> p (w j)").bitcast(F32).rearrange("p (j c) -> p j c", j=4), o[:, 2], nc.sync)
+        finish(3, y[:, 0, :, 0 : M // 4], o[:, 3, 0:1], nc.sync)
+        finish(4, y[:, 1, :, 0 : M // 4], o[:, 3, 1:2], nc.scalar)

@@ -38,7 +38,7 @@ def tile_list_tabx_tm_silu_kernel(tc, tab, w4_words, w4_scales, x, u, b, offs, o
         tab_sc = keep.tile([P, T // 4], I32, name="tab_sc", align_bytes=64)
         picked_sc = keep.tile([P, S], U8, name="picked_sc", align_bytes=64)
         spread = keep.tile([P, (S + M) // 4], I32, name="spread", align_bytes=64)
-        planes = keep.tile([P, A, (S + M) // 4], I32, name="planes", align_bytes=64)
+        plane1 = keep.tile([P, (S + M) // 4], I32, name="plane1", align_bytes=64)
         words = [keep.tile([P, T], I32, name=f"words{a}", align_bytes=64)[:] for a in range(A)]
         w4_w = keep.tile([P, A, 2 * M], U8, name="w4_w", align_bytes=64)
         b_row = keep.tile([P, M], F32, name="b_row", align_bytes=64)
@@ -47,9 +47,12 @@ def tile_list_tabx_tm_silu_kernel(tc, tab, w4_words, w4_scales, x, u, b, offs, o
         warm = keep.tile([P, 1], F32, name="warm", align_bytes=64)
         warm2 = keep.tile([P, 1], F32, name="warm2", align_bytes=64)
 
+        planes = (spread, plane1)
+
         tab_i = tab.bitcast(I32)
         nc.vector.memset(tab_sc[:], 0)
-        nc.vector.memset(planes[:], 0)
+        nc.vector.memset(spread[:, S // 4 :], 0)
+        nc.vector.memset(plane1[:], 0)
         nc.gpsimd.memset(warm[:], 0.0)
         nc.gpsimd.memset(b_row[:], 0.0)
 
@@ -87,8 +90,10 @@ def tile_list_tabx_tm_silu_kernel(tc, tab, w4_words, w4_scales, x, u, b, offs, o
         def place_scales():
             nc.vector.tensor_copy(picked_sc[:], tab_sc[:].bitcast(U8).indirect(offsets[:]))
             nc.vector.tensor_copy(spread[:, 0 : S // 4], picked_sc[:].bitcast(I32))
-            for q in range(4):
-                nc.sync.dma_start(out=planes[32 * q : 32 * q + 4], in_=spread[32 * q : 32 * q + 32 : 4])
+
+        def move_scales(a):
+            for r in range(1 - a, 4):
+                nc.sync.dma_start(out=planes[a][r:P:32], in_=spread[8 * r + 4 * a : P : 32])
 
         load_words(0)
         load_scales()
@@ -99,8 +104,10 @@ def tile_list_tabx_tm_silu_kernel(tc, tab, w4_words, w4_scales, x, u, b, offs, o
         load_x(0, 0, S)
         load_x(1, 0, S)
         place_scales()
+        move_scales(0)
         load_u(0, 2)
         load_words(1)
+        move_scales(1)
         load_u(2, 3)
         for w0 in range(0, S, 256):
             load_x(2, w0, w0 + 256)
@@ -166,7 +173,7 @@ def tile_list_tabx_tm_silu_kernel(tc, tab, w4_words, w4_scales, x, u, b, offs, o
             )
 
         def table_passes(a, w0, w1):
-            plane = planes[:, a, :].bitcast(U8)
+            plane = planes[a][:].bitcast(U8)
             for t in range(w0 // P, w1 // P):
                 mx_pass(t, gw[a], plane, w4_w[:, a, :].bitcast(FP4X4), plane[:, S : S + M])
 

@@ -117,8 +117,8 @@ def tile_list_tabx_tm_silu_kernel(tc, tab, w4_words, w4_scales, x, u, b, offs, o
 
         def interleave(dst, src, w0, w1, by):
             if w1 > w0:
-                o = dst[:, w0:w1, :].rearrange("p (c i) j -> p c j i", i=4)
-                s = src[:, :, w0:w1].rearrange("p j (c i) -> p c j i", i=4)
+                o = dst[:, w0:w1, :].rearrange("p (c i) j -> p c j i", i=2)
+                s = src[:, :, w0:w1].rearrange("p j (c i) -> p c j i", i=2)
                 if by == "S":
                     nc.scalar.copy(o, s)
                 else:

@@ -99,12 +99,12 @@ def tile_list_tabx_tm_silu_kernel(tc, tab, w4_words, w4_scales, x, u, b, offs, o
         load_scales()
         nc.sync.dma_start(offsets[:], offs)
         load_w4_scales()
-        load_w4()
         load_b()
         load_x(0, 0, S)
         load_x(1, 0, S)
         place_scales()
         move_scales(0)
+        load_w4()
         load_u(0, 2)
         load_words(1)
         move_scales(1)
@@ -224,8 +224,8 @@ def tile_list_tabx_tm_silu_kernel(tc, tab, w4_words, w4_scales, x, u, b, offs, o
         gather_words(0, 0, S)
         bias()
         for g in range(2):
-            x_copy(g, 0, 512, 216)
-            x_copy(g, 512, S, 216)
+            x_copy(g, 0, 512, 288)
+            x_copy(g, 512, S, 288)
             quantize(g, 0, 512)
             quantize(g, 512, S)
         table_passes(0, 0, S)

@@ -21,9 +21,8 @@ P = 128
 KP = 512
 A = K // KP
 G = L // KP
-NT = S // P
 BANKS = ((0, 2), (2, 4), (4, 6), (6, 7), (7, 8))
-WIDE = 2
+SCALAR_SHARE = 288
 
 
 def tile_list_tabx_tm_silu_kernel(tc, tab, w4_words, w4_scales, x, u, b, offs, out):
@@ -33,221 +32,211 @@ def tile_list_tabx_tm_silu_kernel(tc, tab, w4_words, w4_scales, x, u, b, offs, o
         keep = ctx.enter_context(tc.tile_pool(name="keep", bufs=1))
         psum = ctx.enter_context(tc.psum_pool(name="psum", bufs=1))
 
+        def sbuf(name, shape, dtype):
+            return keep.tile(shape, dtype, name=name, align_bytes=64)
+
         offsets = keep.tile([P, S // 16], U16, name="offsets")
-        u_raw = keep.tile([P, G, 4, M], F32, name="u_raw", align_bytes=64)
-        tab_sc = keep.tile([P, T // 4], I32, name="tab_sc", align_bytes=64)
-        picked_sc = keep.tile([P, S], U8, name="picked_sc", align_bytes=64)
-        spread = keep.tile([P, (S + M) // 4], I32, name="spread", align_bytes=64)
-        plane1 = keep.tile([P, (S + M) // 4], I32, name="plane1", align_bytes=64)
-        words = [keep.tile([P, T], I32, name=f"words{a}", align_bytes=64)[:] for a in range(A)]
-        w4_w = keep.tile([P, A, 2 * M], U8, name="w4_w", align_bytes=64)
-        b_row = keep.tile([P, M], F32, name="b_row", align_bytes=64)
-        b_col = keep.tile([P, 1], F32, name="b_col", align_bytes=64)
-        ident = keep.tile([P, P], F32, name="ident", align_bytes=64)
-        warm = keep.tile([P, 1], F32, name="warm", align_bytes=64)
-        warm2 = keep.tile([P, 1], F32, name="warm2", align_bytes=64)
+        words = [sbuf(f"words{a}", [P, T], I32) for a in range(A)]
+        tab_sc = sbuf("tab_sc", [P, T // 4], I32)
+        picked_sc = keep.tile([P, S], U8, name="picked_sc", tag="picked0", align_bytes=64)
+        planes = [sbuf(f"plane{a}", [P, (S + M) // 4], I32) for a in range(A)]
+        w4_w = sbuf("w4_w", [P, A, 2 * M], U8)
+        b_row = sbuf("b_row", [P, M], F32)
+        b_col = sbuf("b_col", [P, 1], F32)
+        b_all = sbuf("b_all", [P, 2 * M], F32)
+        ident = sbuf("ident", [P, P], F32)
+        warm_in = sbuf("warm_in", [P, 1], F32)
+        warm_out = sbuf("warm_out", [P, 1], F32)
+        u_first = sbuf("u_first", [P, G - 1, 4, M], F32)
+        u_last = sbuf("u_last", [P, 4, M], F32)
+        u_raw = [u_first[:, 0], u_first[:, 1], u_last[:]]
+        u_bf = sbuf("u_bf", [P, G, M, 4], BF16)
+        u_c = sbuf("u_c", [P, G, M], U32)
+        u_s = sbuf("u_s", [P, G, M], U8)
+        x_c = [sbuf(f"x_c{g}", [P, S], U32) for g in range(G)]
+        x_s = [sbuf(f"x_s{g}", [P, S], U8) for g in range(G)]
+        x_whole = [sbuf(f"x_whole{g}", [P, 4, S], F32) for g in range(G - 1)]
+        raw_a = sbuf("raw_a", [P, 4, 512], F32)
+        raw_b = sbuf("raw_b", [P, 4, 256], F32)
+        raw_c = sbuf("raw_c", [P, 4 * 256 + 128], F32)
 
-        planes = (spread, plane1)
-
-        tab_i = tab.bitcast(I32)
         nc.vector.memset(tab_sc[:], 0)
-        nc.vector.memset(spread[:, S // 4 :], 0)
-        nc.vector.memset(plane1[:], 0)
-        nc.gpsimd.memset(warm[:], 0.0)
+        nc.vector.memset(planes[0][:, S // 4 :], 0)
+        nc.vector.memset(planes[1][:], 0)
+        nc.gpsimd.memset(warm_in[:], 0.0)
         nc.gpsimd.memset(b_row[:], 0.0)
 
+        tab_i = tab.bitcast(I32)
+
         def load_words(a):
-            nc.sync.dma_start(out=words[a], in_=tab_i[a, 0 : 128 * T].rearrange("(p t) -> p t", p=P))
+            nc.sync.dma_start(out=words[a][:], in_=tab_i[a, 0 : 128 * T].rearrange("(p t) -> p t", p=P))
 
-        def load_u(g0, g1):
-            rows = u[KP * g0 : KP * g1, :].rearrange("(g p j) n -> p g j n", p=P, j=4)
-            nc.sync.dma_start(out=u_raw[:, g0:g1], in_=rows)
-
-        x_raw = {}
-
-        def load_x(g, w0, w1):
-            t = keep.tile([P, 4, w1 - w0], F32, name=f"x_raw{g}_{w0}", tag=f"x_raw{g}_{w0}", align_bytes=64)
-            nc.sync.dma_start(out=t[:], in_=x[KP * g : KP * (g + 1), w0:w1].rearrange("(p j) w -> p j w", j=4))
-            for w in range(w0, w1):
-                x_raw[g, w] = (t, w0)
-
-        def load_scales():
-            nc.sync.dma_start(
-                out=tab_sc[0:P:4], in_=tab_i[:, 128 * T : 132 * T].rearrange("a (i t) -> i a t", i=16)
-            )
-
-        def load_w4_scales():
-            nc.sync.dma_start(
-                out=spread[0:P:4, S // 4 :], in_=w4_scales.bitcast(I32).rearrange("a i n -> i a n")
-            )
-
-        def load_w4():
-            nc.sync.dma_start(out=w4_w[:].bitcast(I32), in_=w4_words.bitcast(I32).rearrange("a p n -> p a n"))
-
-        def load_b():
-            nc.sync.dma_start(out=b_row[0:1, :], in_=b.rearrange("(o n) -> o n", o=1))
-
-        def place_scales():
-            nc.vector.tensor_copy(picked_sc[:], tab_sc[:].bitcast(U8).indirect(offsets[:]))
-            nc.vector.tensor_copy(spread[:, 0 : S // 4], picked_sc[:].bitcast(I32))
+        def load_rows(dst, src, g, w0, w1):
+            nc.sync.dma_start(out=dst, in_=src[KP * g : KP * (g + 1), w0:w1].rearrange("(p j) w -> p j w", j=4))
 
         def move_scales(a):
             for r in range(1 - a, 4):
-                nc.sync.dma_start(out=planes[a][r:P:32], in_=spread[8 * r + 4 * a : P : 32])
+                nc.sync.dma_start(out=planes[a][r:P:32], in_=planes[0][8 * r + 4 * a : P : 32])
+
+        view_c = raw_c[:, 0:1024].rearrange("p (j w) -> p j w", j=4)
 
         load_words(0)
-        load_scales()
+        nc.sync.dma_start(out=tab_sc[0:P:4], in_=tab_i[:, 128 * T : 132 * T].rearrange("a (i t) -> i a t", i=16))
         nc.sync.dma_start(offsets[:], offs)
-        load_w4_scales()
-        load_b()
-        load_x(0, 0, S)
-        load_x(1, 0, S)
-        place_scales()
+        nc.sync.dma_start(out=planes[0][0:P:4, S // 4 :], in_=w4_scales.bitcast(I32).rearrange("a i n -> i a n"))
+        nc.sync.dma_start(out=b_row[0:1, :], in_=b.rearrange("(o n) -> o n", o=1))
+        load_rows(x_whole[0][:], x, 0, 0, S)
+        load_rows(x_whole[1][:], x, 1, 0, S)
+        nc.vector.tensor_copy(picked_sc[:], tab_sc[:].bitcast(U8).indirect(offsets[:]))
+        nc.vector.tensor_copy(planes[0][:, 0 : S // 4], picked_sc[:].bitcast(I32))
         move_scales(0)
-        load_w4()
-        load_u(0, 2)
+        nc.sync.dma_start(out=w4_w[:].bitcast(I32), in_=w4_words.bitcast(I32).rearrange("a p n -> p a n"))
+        nc.sync.dma_start(out=u_first[:], in_=u[0 : 2 * KP, :].rearrange("(g p j) n -> p g j n", p=P, j=4))
         load_words(1)
         move_scales(1)
-        load_u(2, 3)
-        for w0 in range(0, S, 256):
-            load_x(2, w0, w0 + 256)
+        load_rows(u_last[:], u, 2, 0, M)
+        load_rows(raw_a[:], x, 2, 0, 512)
+        load_rows(raw_b[:], x, 2, 512, 768)
+        load_rows(view_c, x, 2, 768, S)
 
         make_identity(nc, ident[:])
-        nc.scalar.activation(warm2[:], warm[:], SILU)
+        nc.scalar.activation(warm_out[:], warm_in[:], SILU)
 
-        def interleave(dst, src, w0, w1, by):
-            if w1 > w0:
-                o = dst[:, w0:w1, :].rearrange("p (c i) j -> p c j i", i=2)
-                s = src[:, :, w0:w1].rearrange("p j (c i) -> p c j i", i=2)
-                if by == "S":
-                    nc.scalar.copy(o, s)
-                else:
-                    nc.vector.tensor_copy(o, s)
-
-        u_bf = keep.tile([P, G, M, 4], BF16, name="u_bf", align_bytes=64)
-        u_c = keep.tile([P, G, M], U32, name="u_c", align_bytes=64)
-        u_s = keep.tile([P, G, M], U8, name="u_s", align_bytes=64)
-
-        def u_quantize(g0, g1, by):
-            for g in range(g0, g1):
-                interleave(u_bf[:, g], u_raw[:, g], 0, M, by)
-            nc.vector.quantize_mx(
-                out=u_c[:, g0:g1].rearrange("p g w -> p (g w)").bitcast(FP8X4),
-                scales=u_s[:, g0:g1].rearrange("p g w -> p (g w)"),
-                in_=u_bf[:, g0:g1].rearrange("p g w j -> p (g w j)"),
+        def round_on(copy, dst, src, w0, w1):
+            copy(
+                dst[:, w0:w1, :].rearrange("p (c i) j -> p c j i", i=2),
+                src[:, :, w0:w1].rearrange("p j (c i) -> p c j i", i=2),
             )
 
-        gw = [keep.tile([P, S], U32, name=f"gw{a}", align_bytes=64) for a in range(A)]
+        on_scalar, on_vector = nc.scalar.copy, nc.vector.tensor_copy
 
-        def gather_words(a, w0, w1):
-            nc.vector.tensor_copy(
-                gw[a][:, w0:w1], words[a].bitcast(U32).indirect(offsets[:, w0 // 16 : w1 // 16])
-            )
+        def quantize(codes, scales, rounded):
+            nc.vector.quantize_mx(out=codes.bitcast(FP8X4), scales=scales, in_=rounded.rearrange("p w j -> p (w j)"))
 
-        def bias():
-            b_ps = psum.tile([P, 512], F32, name="b_ps", tag="bank7")
-            nc.tensor.transpose(b_ps[:, 0:P], b_row[:], ident[:])
-            nc.scalar.copy(b_col[:], b_ps[:, 0:1])
-            for s in range(WIDE):
-                nc.tensor.transpose(b_ps[:, P + M * s : P + M * (s + 1)], b_col[:].to_broadcast([P, P]), ident[:])
-            nc.scalar.copy(b_all[:], b_ps[:, P : P + WIDE * M])
+        def quantize_x(g, w0, rounded):
+            w1 = w0 + rounded.shape[1]
+            quantize(x_c[g][:, w0:w1], x_s[g][:, w0:w1], rounded[:])
 
-        b_all = keep.tile([P, WIDE * M], F32, name="b_all", align_bytes=64)
         acc = [psum.tile([P, 512], F32, name=f"acc{i}", tag=f"bank{i}") for i in range(len(BANKS))]
         where = {t: (i, t - t0) for i, (t0, t1) in enumerate(BANKS) for t in range(t0, t1)}
-        passes_done = {i: [] for i in range(len(BANKS))}
+        passes_done = [[] for bank in BANKS]
 
-        def mx_pass(t, codes, scales, w_codes, w_scales):
-            i, s = where[t]
-            c = slice(P * t, P * (t + 1))
-            done = passes_done[i]
-            done.append(t)
-            nc.tensor.matmul_mx(
-                out=acc[i][:, M * s : M * (s + 1)],
-                lhsT=codes[:, c].bitcast(FP8X4),
-                lhsT_scale=scales[:, c],
-                rhs=w_codes,
-                rhs_scale=w_scales,
-                start=(len(done) == 1),
-                stop=(len(done) == (A + G) * (BANKS[i][1] - BANKS[i][0])),
-            )
+        def mx_passes(t0, t1, codes, scales, w_codes, w_scales):
+            for t in range(t0, t1):
+                i, s = where[t]
+                c = slice(P * t, P * (t + 1))
+                passes_done[i].append(t)
+                nc.tensor.matmul_mx(
+                    out=acc[i][:, M * s : M * (s + 1)],
+                    lhsT=codes[:, c].bitcast(FP8X4),
+                    lhsT_scale=scales[:, c],
+                    rhs=w_codes,
+                    rhs_scale=w_scales,
+                    start=(len(passes_done[i]) == 1),
+                    stop=(len(passes_done[i]) == (A + G) * (BANKS[i][1] - BANKS[i][0])),
+                )
 
-        def table_passes(a, w0, w1):
-            plane = planes[a][:].bitcast(U8)
-            for t in range(w0 // P, w1 // P):
-                mx_pass(t, gw[a], plane, w4_w[:, a, :].bitcast(FP4X4), plane[:, S : S + M])
+        def x_passes(g, t0, t1):
+            mx_passes(t0, t1, x_c[g], x_s[g], u_c[:, g].bitcast(FP8X4), u_s[:, g])
 
-        x_bf = {}
-        x_c = [keep.tile([P, S], U32, name=f"x_c{g}", align_bytes=64) for g in range(G)]
-        x_s = [keep.tile([P, S], U8, name=f"x_s{g}", align_bytes=64) for g in range(G)]
-
-        def x_copy(g, w0, w1, sc):
-            raw, load0 = x_raw[g, w0]
-            dst = keep.tile([P, w1 - w0, 4], BF16, name=f"x_bf{g}_{w0}", tag=f"x_bf{g}_{w0}", align_bytes=64)
-            x_bf[g, w0] = dst
-            src = raw[:, :, w0 - load0 : w1 - load0]
-            interleave(dst, src, 0, sc, "S")
-            interleave(dst, src, sc, w1 - w0, "V")
-
-        def quantize(g, w0, w1):
-            nc.vector.quantize_mx(
-                out=x_c[g][:, w0:w1].bitcast(FP8X4),
-                scales=x_s[g][:, w0:w1],
-                in_=x_bf[g, w0][:].rearrange("p w j -> p (w j)"),
-            )
-
-        def x_passes(g, w0, w1):
-            for t in range(w0 // P, w1 // P):
-                mx_pass(t, x_c[g], x_s[g], u_c[:, g].bitcast(FP8X4), u_s[:, g])
-
-        def multiply(g, w0, w1):
-            quantize(g, w0, w1)
-            x_passes(g, w0, w1)
-
-
-        def finish(i, y, o, queue):
-            t0, t1 = BANKS[i]
-            n = M * (t1 - t0)
+        def add_bias(i, y, bias):
+            n = M * (BANKS[i][1] - BANKS[i][0])
             nc.vector.tensor_tensor(
                 y,
                 acc[i][:, 0:n].rearrange("p (j c) -> p j c", j=4),
-                b_all[:, 0:n].rearrange("p (j c) -> p j c", j=4),
+                bias.rearrange("p (j c) -> p j c", j=4),
                 ADD,
             )
-            nc.scalar.activation(
-                o.rearrange("p t (h c) -> p t h c", c=n // 4), y.rearrange("p (t h) c -> p t h c", t=t1 - t0), SILU
-            )
+
+        def activate_and_store(i, o, y, queue):
+            t0, t1 = BANKS[i]
+            nc.scalar.activation(o.rearrange("p (j c) -> p j c", j=4), y, SILU)
             queue.dma_start(
-                out=out[P * t0 : P * t1, :].rearrange("(t p) n -> p t n", p=P), in_=o
+                out=out[P * t0 : P * t1, :].rearrange("(t p) n -> p t n", p=P),
+                in_=o.rearrange("p (t n) -> p t n", n=M),
             )
 
-        gather_words(0, 0, S)
-        bias()
-        for g in range(2):
-            x_copy(g, 0, 512, 288)
-            x_copy(g, 512, S, 288)
-            quantize(g, 0, 512)
-            quantize(g, 512, S)
-        table_passes(0, 0, S)
-        u_quantize(0, 2, "S")
-        x_passes(0, 0, S)
-        x_passes(1, 0, S)
-        gather_words(1, 0, S)
-        table_passes(1, 0, S)
-        u_quantize(2, 3, "S")
-        y = keep.tile([P, 2, 4, WIDE * M // 4], F32, name="y", align_bytes=64)
-        o = keep.tile([P, 4, WIDE, M], F32, name="o", align_bytes=64)
-        for i, share in enumerate((256, 160, 144)):
-            w0 = 256 * i
-            x_copy(2, w0, w0 + 256, share)
-            if i > 1:
-                finish(i - 2, x_raw[2, w0][0][:, :, 192:256], o[:, i - 2], nc.sync)
-            multiply(2, w0, w0 + 256)
-        x_copy(2, 768, 896, 128)
-        x_copy(2, 896, S, 0)
-        finish(1, x_raw[2, 768][0][:, :, 192:256], o[:, 1], nc.sync)
-        multiply(2, 768, 896)
-        multiply(2, 896, S)
-        finish(2, x_bf[2, 896][:].rearrange("p w j -> p (w j)").bitcast(F32).rearrange("p (j c) -> p j c", j=4), o[:, 2], nc.sync)
-        finish(3, y[:, 0, :, 0 : M // 4], o[:, 3, 0:1], nc.sync)
-        finish(4, y[:, 1, :, 0 : M // 4], o[:, 3, 1:2], nc.scalar)
+        def quarters(flat):
+            return flat.rearrange("p (j c) -> p j c", j=4)
+
+        picked = [keep.tile([P, S], U32, name=f"picked{a}", tag=f"picked{a}", align_bytes=64) for a in range(A)]
+
+        def gather_words(a):
+            nc.vector.tensor_copy(picked[a][:], words[a][:].bitcast(U32).indirect(offsets[:]))
+
+        def table_matmuls(a):
+            plane = planes[a][:].bitcast(U8)
+            mx_passes(0, 8, picked[a], plane, w4_w[:, a, :].bitcast(FP4X4), plane[:, S : S + M])
+
+        gather_words(0)
+        b_ps = psum.tile([P, 512], F32, name="b_ps", tag="bank7")
+        nc.tensor.transpose(b_ps[:, 0:P], b_row[:], ident[:])
+        nc.scalar.copy(b_col[:], b_ps[:, 0:1])
+        for s in range(2):
+            nc.tensor.transpose(b_ps[:, P + M * s : P + M * (s + 1)], b_col[:].to_broadcast([P, P]), ident[:])
+        nc.scalar.copy(b_all[:], b_ps[:, P : P + 2 * M])
+
+        def whole_pass(g):
+            halves = [sbuf(f"x_bf{g}_{h}", [P, 512, 4], BF16) for h in range(2)]
+            for h in range(2):
+                src = x_whole[g][:, :, 512 * h : 512 * (h + 1)]
+                round_on(on_scalar, halves[h], src, 0, SCALAR_SHARE)
+                round_on(on_vector, halves[h], src, SCALAR_SHARE, 512)
+            for h in range(2):
+                quantize_x(g, 512 * h, halves[h])
+
+        def u_passes(g0, g1):
+            for g in range(g0, g1):
+                round_on(on_scalar, u_bf[:, g], u_raw[g], 0, M)
+            quantize(
+                u_c[:, g0:g1].rearrange("p g w -> p (g w)"),
+                u_s[:, g0:g1].rearrange("p g w -> p (g w)"),
+                u_bf[:, g0:g1].rearrange("p g w j -> p (g w) j"),
+            )
+
+        whole_pass(0)
+        whole_pass(1)
+        table_matmuls(0)
+        u_passes(0, 2)
+        x_passes(0, 0, 8)
+        x_passes(1, 0, 8)
+        gather_words(1)
+        table_matmuls(1)
+        u_passes(2, 3)
+
+        bf = [sbuf(f"x_bf2_{i}", [P, P * (t1 - t0), 4], BF16) for i, (t0, t1) in enumerate(BANKS)]
+        pair_bias, single_bias = b_all[:], b_all[:, 0:M]
+        o = sbuf("o", [P, 4 * M], F32)
+        y_last = sbuf("y_last", [P, 2, M], F32)
+
+        def multiply(i):
+            t0, t1 = BANKS[i]
+            quantize_x(2, P * t0, bf[i])
+            x_passes(2, t0, t1)
+
+        round_on(on_vector, bf[0], raw_a[:, :, 0:256], 0, 256)
+        round_on(on_vector, bf[1], raw_a[:, :, 256:512], 0, 64)
+        round_on(on_scalar, bf[1], raw_a[:, :, 256:512], 64, 256)
+        multiply(0)
+        multiply(1)
+
+        round_on(on_vector, bf[2], raw_b, 0, 128)
+        round_on(on_scalar, bf[2], raw_b, 128, 256)
+        multiply(2)
+        y0, y1 = raw_b[:, :, 128:192], raw_b[:, :, 192:256]
+        add_bias(0, y0, pair_bias)
+        add_bias(1, y1, pair_bias)
+
+        round_on(on_scalar, bf[4], view_c[:, :, 128:256], 0, 128)
+        round_on(on_vector, bf[3], view_c[:, :, 0:128], 0, 128)
+        activate_and_store(0, raw_c[:, 896:1152], y0, nc.sync)
+        activate_and_store(1, raw_c[:, 640:896], y1, nc.sync)
+        multiply(3)
+        multiply(4)
+        y2 = quarters(raw_c[:, 128:384])
+        add_bias(2, y2, pair_bias)
+        activate_and_store(2, o[:, 0 : 2 * M], y2, nc.sync)
+        add_bias(3, quarters(y_last[:, 0]), single_bias)
+        activate_and_store(3, o[:, 2 * M : 3 * M], quarters(y_last[:, 0]), nc.sync)
+        add_bias(4, quarters(y_last[:, 1]), single_bias)
+        activate_and_store(4, o[:, 3 * M : 4 * M], quarters(y_last[:, 1]), nc.scalar)

@@ -58,7 +58,7 @@ def tile_list_tabx_tm_silu_kernel(tc, tab, w4_words, w4_scales, x, u, b, offs, o
         x_whole = [sbuf(f"x_whole{g}", [P, 4, S], F32) for g in range(G - 1)]
         raw_a = sbuf("raw_a", [P, 4, 512], F32)
         raw_b = sbuf("raw_b", [P, 4, 256], F32)
-        raw_c = sbuf("raw_c", [P, 4 * 256 + 128], F32)
+        raw_c = sbuf("raw_c", [P, 4, 256 + 32], F32)
 
         nc.vector.memset(tab_sc[:], 0)
         nc.vector.memset(planes[0][:, S // 4 :], 0)
@@ -78,8 +78,6 @@ def tile_list_tabx_tm_silu_kernel(tc, tab, w4_words, w4_scales, x, u, b, offs, o
             for r in range(1 - a, 4):
                 nc.sync.dma_start(out=planes[a][r:P:32], in_=planes[0][8 * r + 4 * a : P : 32])
 
-        view_c = raw_c[:, 0:1024].rearrange("p (j w) -> p j w", j=4)
-
         load_words(0)
         nc.sync.dma_start(out=tab_sc[0:P:4], in_=tab_i[:, 128 * T : 132 * T].rearrange("a (i t) -> i a t", i=16))
         nc.sync.dma_start(offsets[:], offs)
@@ -97,7 +95,7 @@ def tile_list_tabx_tm_silu_kernel(tc, tab, w4_words, w4_scales, x, u, b, offs, o
         load_rows(u_last[:], u, 2, 0, M)
         load_rows(raw_a[:], x, 2, 0, 512)
         load_rows(raw_b[:], x, 2, 512, 768)
-        load_rows(view_c, x, 2, 768, S)
+        load_rows(raw_c[:, :, 0:256], x, 2, 768, S)
 
         make_identity(nc, ident[:])
         nc.scalar.activation(warm_out[:], warm_in[:], SILU)
@@ -139,25 +137,25 @@ def tile_list_tabx_tm_silu_kernel(tc, tab, w4_words, w4_scales, x, u, b, offs, o
         def x_passes(g, t0, t1):
             mx_passes(t0, t1, x_c[g], x_s[g], u_c[:, g].bitcast(FP8X4), u_s[:, g])
 
+        def shaped_as(flat, like):
+            if like.ndim == 2:
+                return flat
+            if like.ndim == 3:
+                return flat.rearrange("p (j c) -> p j c", j=like.shape[1])
+            return flat.rearrange("p (t h c) -> p t h c", t=like.shape[1], h=like.shape[2])
+
         def add_bias(i, y, bias):
             n = M * (BANKS[i][1] - BANKS[i][0])
-            nc.vector.tensor_tensor(
-                y,
-                acc[i][:, 0:n].rearrange("p (j c) -> p j c", j=4),
-                bias.rearrange("p (j c) -> p j c", j=4),
-                ADD,
-            )
+            nc.vector.tensor_tensor(y, shaped_as(acc[i][:, 0:n], y), shaped_as(bias, y), ADD)
 
-        def activate_and_store(i, o, y, queue):
+        def activate_and_store(i, results, y, queue):
             t0, t1 = BANKS[i]
-            nc.scalar.activation(o.rearrange("p (j c) -> p j c", j=4), y, SILU)
-            queue.dma_start(
-                out=out[P * t0 : P * t1, :].rearrange("(t p) n -> p t n", p=P),
-                in_=o.rearrange("p (t n) -> p t n", n=M),
-            )
-
-        def quarters(flat):
-            return flat.rearrange("p (j c) -> p j c", j=4)
+            if y.ndim == 2:
+                nc.scalar.activation(results[:, 0], y, SILU)
+            else:
+                runs = y if y.ndim == 4 else y.rearrange("p (t h) c -> p t h c", t=2)
+                nc.scalar.activation(results.rearrange("p t (h c) -> p t h c", h=2), runs, SILU)
+            queue.dma_start(out=out[P * t0 : P * t1, :].rearrange("(t p) n -> p t n", p=P), in_=results)
 
         picked = [keep.tile([P, S], U32, name=f"picked{a}", tag=f"picked{a}", align_bytes=64) for a in range(A)]
 
@@ -206,7 +204,7 @@ def tile_list_tabx_tm_silu_kernel(tc, tab, w4_words, w4_scales, x, u, b, offs, o
 
         bf = [sbuf(f"x_bf2_{i}", [P, P * (t1 - t0), 4], BF16) for i, (t0, t1) in enumerate(BANKS)]
         pair_bias, single_bias = b_all[:], b_all[:, 0:M]
-        o = sbuf("o", [P, 4 * M], F32)
+        o = sbuf("o", [P, 6, M], F32)
         y_last = sbuf("y_last", [P, 2, M], F32)
 
         def multiply(i):
@@ -215,28 +213,29 @@ def tile_list_tabx_tm_silu_kernel(tc, tab, w4_words, w4_scales, x, u, b, offs, o
             x_passes(2, t0, t1)
 
         round_on(on_vector, bf[0], raw_a[:, :, 0:256], 0, 256)
-        round_on(on_vector, bf[1], raw_a[:, :, 256:512], 0, 64)
-        round_on(on_scalar, bf[1], raw_a[:, :, 256:512], 64, 256)
+        round_on(on_scalar, bf[1], raw_a[:, :, 256:512], 0, 256)
         multiply(0)
         multiply(1)
 
-        round_on(on_vector, bf[2], raw_b, 0, 128)
-        round_on(on_scalar, bf[2], raw_b, 128, 256)
-        multiply(2)
-        y0, y1 = raw_b[:, :, 128:192], raw_b[:, :, 192:256]
+        round_on(on_vector, bf[2], raw_b, 0, 64)
+        round_on(on_scalar, bf[2], raw_b, 64, 256)
+        y0 = raw_b[:, :, 0:64]
         add_bias(0, y0, pair_bias)
-        add_bias(1, y1, pair_bias)
+        multiply(2)
 
-        round_on(on_scalar, bf[4], view_c[:, :, 128:256], 0, 128)
-        round_on(on_vector, bf[3], view_c[:, :, 0:128], 0, 128)
-        activate_and_store(0, raw_c[:, 896:1152], y0, nc.sync)
-        activate_and_store(1, raw_c[:, 640:896], y1, nc.sync)
-        multiply(3)
+        round_on(on_vector, bf[4], raw_c[:, :, 128:256], 0, 96)
+        round_on(on_scalar, bf[4], raw_c[:, :, 128:256], 96, 128)
+        round_on(on_scalar, bf[3], raw_c[:, :, 0:128], 0, 128)
+        y1 = raw_c[:, :, 224:288]
+        add_bias(1, y1, pair_bias)
+        activate_and_store(0, raw_c[:, 0:2, 0:M], y0, nc.sync)
+        activate_and_store(1, o[:, 0:2], y1, nc.sync)
         multiply(4)
-        y2 = quarters(raw_c[:, 128:384])
+        multiply(3)
+        y2 = raw_c[:, 2:4, 0:M].rearrange("p t (h c) -> p t h c", h=2)
         add_bias(2, y2, pair_bias)
-        activate_and_store(2, o[:, 0 : 2 * M], y2, nc.sync)
-        add_bias(3, quarters(y_last[:, 0]), single_bias)
-        activate_and_store(3, o[:, 2 * M : 3 * M], quarters(y_last[:, 0]), nc.sync)
-        add_bias(4, quarters(y_last[:, 1]), single_bias)
-        activate_and_store(4, o[:, 3 * M : 4 * M], quarters(y_last[:, 1]), nc.scalar)
+        activate_and_store(2, o[:, 2:4], y2, nc.sync)
+        add_bias(4, y_last[:, 0], single_bias)
+        activate_and_store(4, o[:, 4:5], y_last[:, 0], nc.sync)
+        add_bias(3, y_last[:, 1], single_bias)
+        activate_and_store(3, o[:, 5:6], y_last[:, 1], nc.scalar)

@@ -21,8 +21,9 @@ P = 128
 KP = 512
 A = K // KP
 G = L // KP
-BANKS = ((0, 2), (2, 4), (4, 6), (6, 7), (7, 8))
-SCALAR_SHARE = 288
+BANKS = ((0, 2), (2, 4), (4, 5), (5, 6), (6, 7), (7, 8))
+LAST_SHARE = 136
+SCALAR_SHARE = (288, 224)
 
 
 def tile_list_tabx_tm_silu_kernel(tc, tab, w4_words, w4_scales, x, u, b, offs, out):
@@ -58,7 +59,7 @@ def tile_list_tabx_tm_silu_kernel(tc, tab, w4_words, w4_scales, x, u, b, offs, o
         x_whole = [sbuf(f"x_whole{g}", [P, 4, S], F32) for g in range(G - 1)]
         raw_a = sbuf("raw_a", [P, 4, 512], F32)
         raw_b = sbuf("raw_b", [P, 4, 256], F32)
-        raw_c = sbuf("raw_c", [P, 4, 256 + 32], F32)
+        raw_c = sbuf("raw_c", [P, 4, 256], F32)
 
         nc.vector.memset(tab_sc[:], 0)
         nc.vector.memset(planes[0][:, S // 4 :], 0)
@@ -95,7 +96,7 @@ def tile_list_tabx_tm_silu_kernel(tc, tab, w4_words, w4_scales, x, u, b, offs, o
         load_rows(u_last[:], u, 2, 0, M)
         load_rows(raw_a[:], x, 2, 0, 512)
         load_rows(raw_b[:], x, 2, 512, 768)
-        load_rows(raw_c[:, :, 0:256], x, 2, 768, S)
+        load_rows(raw_c[:], x, 2, 768, S)
 
         make_identity(nc, ident[:])
         nc.scalar.activation(warm_out[:], warm_in[:], SILU)
@@ -113,7 +114,7 @@ def tile_list_tabx_tm_silu_kernel(tc, tab, w4_words, w4_scales, x, u, b, offs, o
 
         def quantize_x(g, w0, rounded):
             w1 = w0 + rounded.shape[1]
-            quantize(x_c[g][:, w0:w1], x_s[g][:, w0:w1], rounded[:])
+            quantize(x_c[g][:, w0:w1], x_s[g][:, w0:w1], rounded)
 
         acc = [psum.tile([P, 512], F32, name=f"acc{i}", tag=f"bank{i}") for i in range(len(BANKS))]
         where = {t: (i, t - t0) for i, (t0, t1) in enumerate(BANKS) for t in range(t0, t1)}
@@ -140,9 +141,7 @@ def tile_list_tabx_tm_silu_kernel(tc, tab, w4_words, w4_scales, x, u, b, offs, o
         def shaped_as(flat, like):
             if like.ndim == 2:
                 return flat
-            if like.ndim == 3:
-                return flat.rearrange("p (j c) -> p j c", j=like.shape[1])
-            return flat.rearrange("p (t h c) -> p t h c", t=like.shape[1], h=like.shape[2])
+            return flat.rearrange("p (j c) -> p j c", j=like.shape[1])
 
         def add_bias(i, y, bias):
             n = M * (BANKS[i][1] - BANKS[i][0])
@@ -153,7 +152,7 @@ def tile_list_tabx_tm_silu_kernel(tc, tab, w4_words, w4_scales, x, u, b, offs, o
             if y.ndim == 2:
                 nc.scalar.activation(results[:, 0], y, SILU)
             else:
-                runs = y if y.ndim == 4 else y.rearrange("p (t h) c -> p t h c", t=2)
+                runs = y.rearrange("p (t h) c -> p t h c", t=2)
                 nc.scalar.activation(results.rearrange("p t (h c) -> p t h c", h=2), runs, SILU)
             queue.dma_start(out=out[P * t0 : P * t1, :].rearrange("(t p) n -> p t n", p=P), in_=results)
 
@@ -178,10 +177,10 @@ def tile_list_tabx_tm_silu_kernel(tc, tab, w4_words, w4_scales, x, u, b, offs, o
             halves = [sbuf(f"x_bf{g}_{h}", [P, 512, 4], BF16) for h in range(2)]
             for h in range(2):
                 src = x_whole[g][:, :, 512 * h : 512 * (h + 1)]
-                round_on(on_scalar, halves[h], src, 0, SCALAR_SHARE)
-                round_on(on_vector, halves[h], src, SCALAR_SHARE, 512)
+                round_on(on_scalar, halves[h], src, 0, SCALAR_SHARE[g])
+                round_on(on_vector, halves[h], src, SCALAR_SHARE[g], 512)
             for h in range(2):
-                quantize_x(g, 512 * h, halves[h])
+                quantize_x(g, 512 * h, halves[h][:])
 
         def u_passes(g0, g1):
             for g in range(g0, g1):
@@ -202,40 +201,40 @@ def tile_list_tabx_tm_silu_kernel(tc, tab, w4_words, w4_scales, x, u, b, offs, o
         table_matmuls(1)
         u_passes(2, 3)
 
-        bf = [sbuf(f"x_bf2_{i}", [P, P * (t1 - t0), 4], BF16) for i, (t0, t1) in enumerate(BANKS)]
+        bf_a = [sbuf(f"x_bf2_a{h}", [P, 256, 4], BF16) for h in range(2)]
+        bf_b = [sbuf(f"x_bf2_b{h}", [P, 128, 4], BF16) for h in range(2)]
+        bf_c = sbuf("x_bf2_c", [P, 256, 4], BF16)
+        rounded = [bf_a[0][:], bf_a[1][:], bf_b[0][:], bf_b[1][:], bf_c[:, 0:128], bf_c[:, 128:256]]
         pair_bias, single_bias = b_all[:], b_all[:, 0:M]
-        o = sbuf("o", [P, 6, M], F32)
+        o = sbuf("o", [P, 4, M], F32)
+        y_first = sbuf("y_first", [P, 4, 64], F32)
         y_last = sbuf("y_last", [P, 2, M], F32)
 
         def multiply(i):
             t0, t1 = BANKS[i]
-            quantize_x(2, P * t0, bf[i])
+            quantize_x(2, P * t0, rounded[i])
             x_passes(2, t0, t1)
 
-        round_on(on_vector, bf[0], raw_a[:, :, 0:256], 0, 256)
-        round_on(on_scalar, bf[1], raw_a[:, :, 256:512], 0, 256)
+        round_on(on_vector, bf_a[0], raw_a[:, :, 0:256], 0, 256)
+        round_on(on_scalar, bf_a[1], raw_a[:, :, 256:512], 0, 256)
         multiply(0)
         multiply(1)
+        add_bias(0, y_first[:], pair_bias)
 
-        round_on(on_vector, bf[2], raw_b, 0, 64)
-        round_on(on_scalar, bf[2], raw_b, 64, 256)
-        y0 = raw_b[:, :, 0:64]
-        add_bias(0, y0, pair_bias)
+        round_on(on_scalar, bf_b[0], raw_b[:, :, 0:128], 0, 128)
+        round_on(on_scalar, bf_b[1], raw_b[:, :, 128:256], 0, 128)
         multiply(2)
-
-        round_on(on_vector, bf[4], raw_c[:, :, 128:256], 0, 96)
-        round_on(on_scalar, bf[4], raw_c[:, :, 128:256], 96, 128)
-        round_on(on_scalar, bf[3], raw_c[:, :, 0:128], 0, 128)
-        y1 = raw_c[:, :, 224:288]
-        add_bias(1, y1, pair_bias)
-        activate_and_store(0, raw_c[:, 0:2, 0:M], y0, nc.sync)
-        activate_and_store(1, o[:, 0:2], y1, nc.sync)
-        multiply(4)
+        y_second = raw_b[:, :, 0:64]
+        add_bias(1, y_second, pair_bias)
         multiply(3)
-        y2 = raw_c[:, 2:4, 0:M].rearrange("p t (h c) -> p t h c", h=2)
-        add_bias(2, y2, pair_bias)
-        activate_and_store(2, o[:, 2:4], y2, nc.sync)
-        add_bias(4, y_last[:, 0], single_bias)
-        activate_and_store(4, o[:, 4:5], y_last[:, 0], nc.sync)
-        add_bias(3, y_last[:, 1], single_bias)
-        activate_and_store(3, o[:, 5:6], y_last[:, 1], nc.scalar)
+
+        round_on(on_scalar, bf_c, raw_c, 0, LAST_SHARE)
+        round_on(on_vector, bf_c, raw_c, LAST_SHARE, 256)
+        activate_and_store(0, raw_c[:, 0:2, 0:M], y_first[:], nc.sync)
+        activate_and_store(1, raw_c[:, 2:4, 0:M], y_second, nc.sync)
+        multiply(4)
+        multiply(5)
+        sums = [raw_c[:, 0, M : 2 * M], raw_c[:, 1, M : 2 * M], y_last[:, 0], y_last[:, 1]]
+        for n, y in enumerate(sums):
+            add_bias(2 + n, y, single_bias)
+            activate_and_store(2 + n, o[:, n : n + 1], y, nc.scalar if n == 3 else nc.sync)

@@ -103,8 +103,8 @@ def tile_list_tabx_tm_silu_kernel(tc, tab, w4_words, w4_scales, x, u, b, offs, o
 
         def round_on(copy, dst, src, w0, w1):
             copy(
-                dst[:, w0:w1, :].rearrange("p (c i) j -> p c j i", i=2),
-                src[:, :, w0:w1].rearrange("p j (c i) -> p c j i", i=2),
+                dst[:, w0:w1, :].rearrange("p (c i) j -> p c j i", i=4),
+                src[:, :, w0:w1].rearrange("p j (c i) -> p c j i", i=4),
             )
 
         on_scalar, on_vector = nc.scalar.copy, nc.vector.tensor_copy

@@ -24,6 +24,7 @@ G = L // KP
 BANKS = ((0, 2), (2, 4), (4, 5), (5, 6), (6, 7), (7, 8))
 LAST_SHARE = 136
 SCALAR_SHARE = (288, 224)
+FIRST_SHARE = 224
 
 
 def tile_list_tabx_tm_silu_kernel(tc, tab, w4_words, w4_scales, x, u, b, offs, out):
@@ -89,25 +90,29 @@ def tile_list_tabx_tm_silu_kernel(tc, tab, w4_words, w4_scales, x, u, b, offs, o
         nc.vector.tensor_copy(picked_sc[:], tab_sc[:].bitcast(U8).indirect(offsets[:]))
         nc.vector.tensor_copy(planes[0][:, 0 : S // 4], picked_sc[:].bitcast(I32))
         move_scales(0)
-        nc.sync.dma_start(out=w4_w[:].bitcast(I32), in_=w4_words.bitcast(I32).rearrange("a p n -> p a n"))
         nc.sync.dma_start(out=u_first[:], in_=u[0 : 2 * KP, :].rearrange("(g p j) n -> p g j n", p=P, j=4))
         load_words(1)
-        move_scales(1)
         load_rows(u_last[:], u, 2, 0, M)
         load_rows(raw_a[:], x, 2, 0, 512)
+        move_scales(1)
+        nc.sync.dma_start(out=w4_w[:].bitcast(I32), in_=w4_words.bitcast(I32).rearrange("a p n -> p a n"))
         load_rows(raw_b[:], x, 2, 512, 768)
         load_rows(raw_c[:], x, 2, 768, S)
 
         make_identity(nc, ident[:])
         nc.scalar.activation(warm_out[:], warm_in[:], SILU)
 
-        def round_on(copy, dst, src, w0, w1):
-            copy(
-                dst[:, w0:w1, :].rearrange("p (c i) j -> p c j i", i=4),
-                src[:, :, w0:w1].rearrange("p j (c i) -> p c j i", i=4),
+        def on_scalar(dst, src):
+            nc.scalar.copy(dst.rearrange("p (c i) j -> p c j i", i=4), src.rearrange("p j (c i) -> p c j i", i=4))
+
+        def on_vector(dst, src):
+            nc.vector.tensor_copy(
+                dst.rearrange("p (c i) (h l) -> p c h i l", i=4, l=2),
+                src.rearrange("p (h l) (c i) -> p c h i l", i=4, l=2),
             )
 
-        on_scalar, on_vector = nc.scalar.copy, nc.vector.tensor_copy
+        def round_on(copy, dst, src, w0, w1):
+            copy(dst[:, w0:w1, :], src[:, :, w0:w1])
 
         def quantize(codes, scales, rounded):
             nc.vector.quantize_mx(out=codes.bitcast(FP8X4), scales=scales, in_=rounded.rearrange("p w j -> p (w j)"))
@@ -153,7 +158,7 @@ def tile_list_tabx_tm_silu_kernel(tc, tab, w4_words, w4_scales, x, u, b, offs, o
                 nc.scalar.activation(results[:, 0], y, SILU)
             else:
                 runs = y.rearrange("p (t h) c -> p t h c", t=2)
-                nc.scalar.activation(results.rearrange("p t (h c) -> p t h c", h=2), runs, SILU)
+                nc.scalar.activation(results.rearrange("p t (h c) -> p t h c", c=y.shape[2]), runs, SILU)
             queue.dma_start(out=out[P * t0 : P * t1, :].rearrange("(t p) n -> p t n", p=P), in_=results)
 
         picked = [keep.tile([P, S], U32, name=f"picked{a}", tag=f"picked{a}", align_bytes=64) for a in range(A)]
@@ -161,9 +166,10 @@ def tile_list_tabx_tm_silu_kernel(tc, tab, w4_words, w4_scales, x, u, b, offs, o
         def gather_words(a):
             nc.vector.tensor_copy(picked[a][:], words[a][:].bitcast(U32).indirect(offsets[:]))
 
-        def table_matmuls(a):
-            plane = planes[a][:].bitcast(U8)
-            mx_passes(0, 8, picked[a], plane, w4_w[:, a, :].bitcast(FP4X4), plane[:, S : S + M])
+        def table_passes(t0, t1):
+            for a in range(A):
+                plane = planes[a][:].bitcast(U8)
+                mx_passes(t0, t1, picked[a], plane, w4_w[:, a, :].bitcast(FP4X4), plane[:, S : S + M])
 
         gather_words(0)
         b_ps = psum.tile([P, 512], F32, name="b_ps", tag="bank7")
@@ -193,12 +199,10 @@ def tile_list_tabx_tm_silu_kernel(tc, tab, w4_words, w4_scales, x, u, b, offs, o
 
         whole_pass(0)
         whole_pass(1)
-        table_matmuls(0)
         u_passes(0, 2)
         x_passes(0, 0, 8)
         x_passes(1, 0, 8)
         gather_words(1)
-        table_matmuls(1)
         u_passes(2, 3)
 
         bf_a = [sbuf(f"x_bf2_a{h}", [P, 256, 4], BF16) for h in range(2)]
@@ -215,15 +219,20 @@ def tile_list_tabx_tm_silu_kernel(tc, tab, w4_words, w4_scales, x, u, b, offs, o
             quantize_x(2, P * t0, rounded[i])
             x_passes(2, t0, t1)
 
-        round_on(on_vector, bf_a[0], raw_a[:, :, 0:256], 0, 256)
+        round_on(on_vector, bf_a[0], raw_a[:, :, 0:256], 0, FIRST_SHARE)
+        round_on(on_scalar, bf_a[0], raw_a[:, :, 0:256], FIRST_SHARE, 256)
         round_on(on_scalar, bf_a[1], raw_a[:, :, 256:512], 0, 256)
+        table_passes(0, 2)
         multiply(0)
+        table_passes(2, 4)
         multiply(1)
+        table_passes(4, 6)
         add_bias(0, y_first[:], pair_bias)
 
         round_on(on_scalar, bf_b[0], raw_b[:, :, 0:128], 0, 128)
         round_on(on_scalar, bf_b[1], raw_b[:, :, 128:256], 0, 128)
         multiply(2)
+        table_passes(6, 8)
         y_second = raw_b[:, :, 0:64]
         add_bias(1, y_second, pair_bias)
         multiply(3)

@@ -23,7 +23,7 @@ A = K // KP
 G = L // KP
 BANKS = ((0, 2), (2, 4), (4, 5), (5, 6), (6, 7), (7, 8))
 LAST_SHARE = 136
-SCALAR_SHARE = (288, 224)
+SCALAR_SHARE = (352, 224)
 FIRST_SHARE = 224
 
 

@@ -47,7 +47,6 @@ def tile_list_tabx_tm_silu_kernel(tc, tab, w4_words, w4_scales, x, u, b, offs, o
         b_col = sbuf("b_col", [P, 1], F32)
         b_all = sbuf("b_all", [P, 2 * M], F32)
         ident = sbuf("ident", [P, P], F32)
-        warm_in = sbuf("warm_in", [P, 1], F32)
         warm_out = sbuf("warm_out", [P, 1], F32)
         u_first = sbuf("u_first", [P, G - 1, 4, M], F32)
         u_last = sbuf("u_last", [P, 4, M], F32)
@@ -65,7 +64,6 @@ def tile_list_tabx_tm_silu_kernel(tc, tab, w4_words, w4_scales, x, u, b, offs, o
         nc.vector.memset(tab_sc[:], 0)
         nc.vector.memset(planes[0][:, S // 4 :], 0)
         nc.vector.memset(planes[1][:], 0)
-        nc.gpsimd.memset(warm_in[:], 0.0)
         nc.gpsimd.memset(b_row[:], 0.0)
 
         tab_i = tab.bitcast(I32)
@@ -100,7 +98,7 @@ def tile_list_tabx_tm_silu_kernel(tc, tab, w4_words, w4_scales, x, u, b, offs, o
         load_rows(raw_c[:], x, 2, 768, S)
 
         make_identity(nc, ident[:])
-        nc.scalar.activation(warm_out[:], warm_in[:], SILU)
+        nc.scalar.activation(warm_out[:], ident[:, 0:1], SILU)
 
         def on_scalar(dst, src):
             nc.scalar.copy(dst.rearrange("p (c i) j -> p c j i", i=4), src.rearrange("p j (c i) -> p c j i", i=4))

@@ -24,7 +24,7 @@ G = L // KP
 BANKS = ((0, 2), (2, 4), (4, 5), (5, 6), (6, 7), (7, 8))
 LAST_SHARE = 136
 SCALAR_SHARE = (352, 224)
-FIRST_SHARE = 224
+SECOND_SHARE = 192
 
 
 def tile_list_tabx_tm_silu_kernel(tc, tab, w4_words, w4_scales, x, u, b, offs, out):
@@ -217,9 +217,10 @@ def tile_list_tabx_tm_silu_kernel(tc, tab, w4_words, w4_scales, x, u, b, offs, o
             quantize_x(2, P * t0, rounded[i])
             x_passes(2, t0, t1)
 
-        round_on(on_vector, bf_a[0], raw_a[:, :, 0:256], 0, FIRST_SHARE)
-        round_on(on_scalar, bf_a[0], raw_a[:, :, 0:256], FIRST_SHARE, 256)
-        round_on(on_scalar, bf_a[1], raw_a[:, :, 256:512], 0, 256)
+        round_on(on_vector, bf_a[0], raw_a[:, :, 0:256], 0, P)
+        round_on(on_scalar, bf_a[0], raw_a[:, :, 0:256], P, 256)
+        round_on(on_vector, bf_a[1], raw_a[:, :, 256:512], SECOND_SHARE, 256)
+        round_on(on_scalar, bf_a[1], raw_a[:, :, 256:512], 0, SECOND_SHARE)
         table_passes(0, 2)
         multiply(0)
         table_passes(2, 4)

from contextlib import ExitStack

import concourse.mybir as mybir
from concourse.masks import make_identity

K, L, M, T, S = 1024, 1536, 128, 2048, 1024
FLOPS = 2 * S * M * (K + L)

F32 = mybir.dt.float32
BF16 = mybir.dt.bfloat16
I32 = mybir.dt.int32
U32 = mybir.dt.uint32
U16 = mybir.dt.uint16
U8 = mybir.dt.uint8
FP8X4 = mybir.dt.float8_e4m3fn_x4
FP4X4 = mybir.dt.float4_e2m1fn_x4
SILU = mybir.ActivationFunctionType.Silu
ADD = mybir.AluOpType.add

P = 128
KP = 512
A = K // KP
G = L // KP
BANKS = ((0, 2), (2, 4), (4, 5), (5, 6), (6, 7), (7, 8))
LAST_SHARE = 136
SCALAR_SHARE = (352, 224)
SECOND_SHARE = 192


def tile_list_tabx_tm_silu_kernel(tc, tab, w4_words, w4_scales, x, u, b, offs, out):
    nc = tc.nc

    with ExitStack() as ctx:
        keep = ctx.enter_context(tc.tile_pool(name="keep", bufs=1))
        psum = ctx.enter_context(tc.psum_pool(name="psum", bufs=1))

        def sbuf(name, shape, dtype):
            return keep.tile(shape, dtype, name=name, align_bytes=64)

        offsets = keep.tile([P, S // 16], U16, name="offsets")
        words = [sbuf(f"words{a}", [P, T], I32) for a in range(A)]
        tab_sc = sbuf("tab_sc", [P, T // 4], I32)
        picked_sc = keep.tile([P, S], U8, name="picked_sc", tag="picked0", align_bytes=64)
        planes = [sbuf(f"plane{a}", [P, (S + M) // 4], I32) for a in range(A)]
        w4_w = sbuf("w4_w", [P, A, 2 * M], U8)
        b_row = sbuf("b_row", [P, M], F32)
        b_col = sbuf("b_col", [P, 1], F32)
        b_all = sbuf("b_all", [P, 2 * M], F32)
        ident = sbuf("ident", [P, P], F32)
        warm_out = sbuf("warm_out", [P, 1], F32)
        u_first = sbuf("u_first", [P, G - 1, 4, M], F32)
        u_last = sbuf("u_last", [P, 4, M], F32)
        u_raw = [u_first[:, 0], u_first[:, 1], u_last[:]]
        u_bf = sbuf("u_bf", [P, G, M, 4], BF16)
        u_c = sbuf("u_c", [P, G, M], U32)
        u_s = sbuf("u_s", [P, G, M], U8)
        x_c = [sbuf(f"x_c{g}", [P, S], U32) for g in range(G)]
        x_s = [sbuf(f"x_s{g}", [P, S], U8) for g in range(G)]
        x_whole = [sbuf(f"x_whole{g}", [P, 4, S], F32) for g in range(G - 1)]
        raw_a = sbuf("raw_a", [P, 4, 512], F32)
        raw_b = sbuf("raw_b", [P, 4, 256], F32)
        raw_c = sbuf("raw_c", [P, 4, 256], F32)

        nc.vector.memset(tab_sc[:], 0)
        nc.vector.memset(planes[0][:, S // 4 :], 0)
        nc.vector.memset(planes[1][:], 0)
        nc.gpsimd.memset(b_row[:], 0.0)

        tab_i = tab.bitcast(I32)

        def load_words(a):
            nc.sync.dma_start(out=words[a][:], in_=tab_i[a, 0 : 128 * T].rearrange("(p t) -> p t", p=P))

        def load_rows(dst, src, g, w0, w1):
            nc.sync.dma_start(out=dst, in_=src[KP * g : KP * (g + 1), w0:w1].rearrange("(p j) w -> p j w", j=4))

        def move_scales(a):
            for r in range(1 - a, 4):
                nc.sync.dma_start(out=planes[a][r:P:32], in_=planes[0][8 * r + 4 * a : P : 32])

        load_words(0)
        nc.sync.dma_start(out=tab_sc[0:P:4], in_=tab_i[:, 128 * T : 132 * T].rearrange("a (i t) -> i a t", i=16))
        nc.sync.dma_start(offsets[:], offs)
        nc.sync.dma_start(out=planes[0][0:P:4, S // 4 :], in_=w4_scales.bitcast(I32).rearrange("a i n -> i a n"))
        nc.sync.dma_start(out=b_row[0:1, :], in_=b.rearrange("(o n) -> o n", o=1))
        load_rows(x_whole[0][:], x, 0, 0, S)
        load_rows(x_whole[1][:], x, 1, 0, S)
        nc.vector.tensor_copy(picked_sc[:], tab_sc[:].bitcast(U8).indirect(offsets[:]))
        nc.vector.tensor_copy(planes[0][:, 0 : S // 4], picked_sc[:].bitcast(I32))
        move_scales(0)
        nc.sync.dma_start(out=u_first[:], in_=u[0 : 2 * KP, :].rearrange("(g p j) n -> p g j n", p=P, j=4))
        load_words(1)
        load_rows(u_last[:], u, 2, 0, M)
        load_rows(raw_a[:], x, 2, 0, 512)
        move_scales(1)
        nc.sync.dma_start(out=w4_w[:].bitcast(I32), in_=w4_words.bitcast(I32).rearrange("a p n -> p a n"))
        load_rows(raw_b[:], x, 2, 512, 768)
        load_rows(raw_c[:], x, 2, 768, S)

        make_identity(nc, ident[:])
        nc.scalar.activation(warm_out[:], ident[:, 0:1], SILU)

        def on_scalar(dst, src):
            nc.scalar.copy(dst.rearrange("p (c i) j -> p c j i", i=4), src.rearrange("p j (c i) -> p c j i", i=4))

        def on_vector(dst, src):
            nc.vector.tensor_copy(
                dst.rearrange("p (c i) (h l) -> p c h i l", i=4, l=2),
                src.rearrange("p (h l) (c i) -> p c h i l", i=4, l=2),
            )

        def round_on(copy, dst, src, w0, w1):
            copy(dst[:, w0:w1, :], src[:, :, w0:w1])

        def quantize(codes, scales, rounded):
            nc.vector.quantize_mx(out=codes.bitcast(FP8X4), scales=scales, in_=rounded.rearrange("p w j -> p (w j)"))

        def quantize_x(g, w0, rounded):
            w1 = w0 + rounded.shape[1]
            quantize(x_c[g][:, w0:w1], x_s[g][:, w0:w1], rounded)

        acc = [psum.tile([P, 512], F32, name=f"acc{i}", tag=f"bank{i}") for i in range(len(BANKS))]
        where = {t: (i, t - t0) for i, (t0, t1) in enumerate(BANKS) for t in range(t0, t1)}
        passes_done = [[] for bank in BANKS]

        def mx_passes(t0, t1, codes, scales, w_codes, w_scales):
            for t in range(t0, t1):
                i, s = where[t]
                c = slice(P * t, P * (t + 1))
                passes_done[i].append(t)
                nc.tensor.matmul_mx(
                    out=acc[i][:, M * s : M * (s + 1)],
                    lhsT=codes[:, c].bitcast(FP8X4),
                    lhsT_scale=scales[:, c],
                    rhs=w_codes,
                    rhs_scale=w_scales,
                    start=(len(passes_done[i]) == 1),
                    stop=(len(passes_done[i]) == (A + G) * (BANKS[i][1] - BANKS[i][0])),
                )

        def x_passes(g, t0, t1):
            mx_passes(t0, t1, x_c[g], x_s[g], u_c[:, g].bitcast(FP8X4), u_s[:, g])

        def shaped_as(flat, like):
            if like.ndim == 2:
                return flat
            return flat.rearrange("p (j c) -> p j c", j=like.shape[1])

        def add_bias(i, y, bias):
            n = M * (BANKS[i][1] - BANKS[i][0])
            nc.vector.tensor_tensor(y, shaped_as(acc[i][:, 0:n], y), shaped_as(bias, y), ADD)

        def activate_and_store(i, results, y, queue):
            t0, t1 = BANKS[i]
            if y.ndim == 2:
                nc.scalar.activation(results[:, 0], y, SILU)
            else:
                runs = y.rearrange("p (t h) c -> p t h c", t=2)
                nc.scalar.activation(results.rearrange("p t (h c) -> p t h c", c=y.shape[2]), runs, SILU)
            queue.dma_start(out=out[P * t0 : P * t1, :].rearrange("(t p) n -> p t n", p=P), in_=results)

        picked = [keep.tile([P, S], U32, name=f"picked{a}", tag=f"picked{a}", align_bytes=64) for a in range(A)]

        def gather_words(a):
            nc.vector.tensor_copy(picked[a][:], words[a][:].bitcast(U32).indirect(offsets[:]))

        def table_passes(t0, t1):
            for a in range(A):
                plane = planes[a][:].bitcast(U8)
                mx_passes(t0, t1, picked[a], plane, w4_w[:, a, :].bitcast(FP4X4), plane[:, S : S + M])

        gather_words(0)
        b_ps = psum.tile([P, 512], F32, name="b_ps", tag="bank7")
        nc.tensor.transpose(b_ps[:, 0:P], b_row[:], ident[:])
        nc.scalar.copy(b_col[:], b_ps[:, 0:1])
        for s in range(2):
            nc.tensor.transpose(b_ps[:, P + M * s : P + M * (s + 1)], b_col[:].to_broadcast([P, P]), ident[:])
        nc.scalar.copy(b_all[:], b_ps[:, P : P + 2 * M])

        def whole_pass(g):
            halves = [sbuf(f"x_bf{g}_{h}", [P, 512, 4], BF16) for h in range(2)]
            for h in range(2):
                src = x_whole[g][:, :, 512 * h : 512 * (h + 1)]
                round_on(on_scalar, halves[h], src, 0, SCALAR_SHARE[g])
                round_on(on_vector, halves[h], src, SCALAR_SHARE[g], 512)
            for h in range(2):
                quantize_x(g, 512 * h, halves[h][:])

        def u_passes(g0, g1):
            for g in range(g0, g1):
                round_on(on_scalar, u_bf[:, g], u_raw[g], 0, M)
            quantize(
                u_c[:, g0:g1].rearrange("p g w -> p (g w)"),
                u_s[:, g0:g1].rearrange("p g w -> p (g w)"),
                u_bf[:, g0:g1].rearrange("p g w j -> p (g w) j"),
            )

        whole_pass(0)
        whole_pass(1)
        u_passes(0, 2)
        x_passes(0, 0, 8)
        x_passes(1, 0, 8)
        gather_words(1)
        u_passes(2, 3)

        bf_a = [sbuf(f"x_bf2_a{h}", [P, 256, 4], BF16) for h in range(2)]
        bf_b = [sbuf(f"x_bf2_b{h}", [P, 128, 4], BF16) for h in range(2)]
        bf_c = sbuf("x_bf2_c", [P, 256, 4], BF16)
        rounded = [bf_a[0][:], bf_a[1][:], bf_b[0][:], bf_b[1][:], bf_c[:, 0:128], bf_c[:, 128:256]]
        pair_bias, single_bias = b_all[:], b_all[:, 0:M]
        o = sbuf("o", [P, 4, M], F32)
        y_first = sbuf("y_first", [P, 4, 64], F32)
        y_last = sbuf("y_last", [P, 2, M], F32)

        def multiply(i):
            t0, t1 = BANKS[i]
            quantize_x(2, P * t0, rounded[i])
            x_passes(2, t0, t1)

        round_on(on_vector, bf_a[0], raw_a[:, :, 0:256], 0, P)
        round_on(on_scalar, bf_a[0], raw_a[:, :, 0:256], P, 256)
        round_on(on_vector, bf_a[1], raw_a[:, :, 256:512], SECOND_SHARE, 256)
        round_on(on_scalar, bf_a[1], raw_a[:, :, 256:512], 0, SECOND_SHARE)
        table_passes(0, 2)
        multiply(0)
        table_passes(2, 4)
        multiply(1)
        table_passes(4, 6)
        add_bias(0, y_first[:], pair_bias)

        round_on(on_scalar, bf_b[0], raw_b[:, :, 0:128], 0, 128)
        round_on(on_scalar, bf_b[1], raw_b[:, :, 128:256], 0, 128)
        multiply(2)
        table_passes(6, 8)
        y_second = raw_b[:, :, 0:64]
        add_bias(1, y_second, pair_bias)
        multiply(3)

        round_on(on_scalar, bf_c, raw_c, 0, LAST_SHARE)
        round_on(on_vector, bf_c, raw_c, LAST_SHARE, 256)
        activate_and_store(0, raw_c[:, 0:2, 0:M], y_first[:], nc.sync)
        activate_and_store(1, raw_c[:, 2:4, 0:M], y_second, nc.sync)
        multiply(4)
        multiply(5)
        sums = [raw_c[:, 0, M : 2 * M], raw_c[:, 1, M : 2 * M], y_last[:, 0], y_last[:, 1]]
        for n, y in enumerate(sums):
            add_bias(2 + n, y, single_bias)
            activate_and_store(2 + n, o[:, n : n + 1], y, nc.scalar if n == 3 else nc.sync)
